import numpy as np
import ml_dtypes


def mxq(x, axis, fmt="e4m3"):
    dtype, down = {"e4m3": (ml_dtypes.float8_e4m3fn, 7), "e5m2": (ml_dtypes.float8_e5m2, 14)}[fmt]
    v = np.moveaxis(np.asarray(x, np.float32).astype(ml_dtypes.bfloat16).astype(np.float64), axis, -1)
    blocks = v.reshape(v.shape[:-1] + (-1, 32))
    amax = np.abs(blocks).max(-1, keepdims=True)
    byte = np.maximum(np.where(amax > 0, np.frexp(amax)[1] - 1 + 127, 0) - down, 1)
    scale = np.exp2(byte - 127.0)
    codes = (blocks / scale).astype(np.float32).astype(dtype).astype(np.float64)
    return np.moveaxis((codes * scale).reshape(v.shape), -1, axis)


WIDE = False


def mx_kscale(k):
    if not WIDE:
        return np.ones(k)
    levels = np.array([10, -10, 5, -5, 0])
    if k % 512:
        return np.exp2(np.random.permutation(np.resize(levels, k // 32))).repeat(32)
    a = np.empty((k // 512, 16))
    for p in range(k // 512):
        a[p, :8] = np.random.permutation(np.resize(levels, 8))
        for g in range(8):
            far = levels[np.abs(levels - a[p, g]) >= 10]
            a[p, g + 8] = far[np.random.randint(len(far))]
    return np.exp2(a.ravel()).repeat(32)


def f64(x):
    return np.asarray(x).astype(np.float64)


def striped(idx):
    return np.tile(idx.reshape(-1, 16).T, (8, 1)).astype(np.uint16)


def unstriped(offs):
    return offs[:16].T.reshape(-1).astype(np.int64)


def pack_weight(w):
    k, n = w.shape
    w = f64(np.asarray(w, np.float32).astype(ml_dtypes.bfloat16)).reshape(k // 32, 32, n)
    amax = np.abs(w).max(1)
    byte = np.clip(np.where(amax > 0, np.frexp(amax)[1] - 1 + 127 - 7, 1), 1, 254)
    scaled = (w * np.exp2(127.0 - byte)[:, None, :]).reshape(k, n).astype(np.float32)
    words = np.ascontiguousarray(scaled.reshape(k // 512, 128, 4, n).transpose(0, 1, 3, 2)).astype(ml_dtypes.float8_e4m3fn).view(np.uint8)
    return words, np.ascontiguousarray(byte.astype(np.uint8).reshape(k // 512, 16, n))


def unpack_weight(words, scales):
    g, p, n, _ = words.shape
    vals = np.ascontiguousarray(words).view(ml_dtypes.float8_e4m3fn).astype(np.float64) * np.repeat(np.exp2(scales.astype(np.float64) - 127.0), 8, axis=1)[..., None]
    return vals.transpose(0, 1, 3, 2).reshape(g * 512, n)


def silu(v):
    return v / (1.0 + np.exp(-np.maximum(v, -700.0)))


K, T, S, H, N, U = 1024, 1024, 512, 512, 128, 1024
P = 2 ** 7


def setup_inputs():
    n = np.random.standard_normal
    s = mx_kscale(K)[:, None]
    u = mx_kscale(H)
    packed_w2 = pack_weight(n((H, N)) / np.sqrt(H) / u[:, None])
    return {
        "xT": (n((K, T)) * s).astype(np.float32),
        "gate": np.tile(np.random.uniform(0.5, 1.5, S), (P, 1)).astype(np.float32),
        "w1": (n((K, H)) / np.sqrt(K) / s).astype(np.float32),
        "w3": (n((K, H)) / np.sqrt(K) / s * u).astype(np.float32),
        "w2_words": packed_w2[0],
        "w2_scales": packed_w2[1],
        "offs": striped(np.random.permutation(T)[:S]),
        "dst": striped(np.random.permutation(U)[:S]),
    }


def reference(xT, gate, w1, w3, w2_words, w2_scales, offs, dst):
    xq = mxq(f64(xT)[:, unstriped(offs)], 0, "e4m3")
    h = (silu(mxq(f64(w1), 0, "e4m3").T @ xq)) * ((mxq(f64(w3), 0, "e4m3").T @ xq))
    y = unpack_weight(w2_words, w2_scales).T @ mxq(h, 0, "e4m3")
    out = np.zeros((N, U))
    out[:, unstriped(dst)] = y * f64(gate)[:1]
    return out

@@ -1,0 +1,225 @@
+from contextlib import ExitStack
+
+import concourse.mybir as mybir
+
+K, T, S, H, N, U = 1024, 1024, 512, 512, 128, 1024
+FLOPS = 2 * S * (2 * K * H + H * N)
+
+F32 = mybir.dt.float32
+BF16 = mybir.dt.bfloat16
+I32 = mybir.dt.int32
+U32 = mybir.dt.uint32
+U16 = mybir.dt.uint16
+U8 = mybir.dt.uint8
+FP8X4 = mybir.dt.float8_e4m3fn_x4
+MULT = mybir.AluOpType.mult
+SILU = mybir.ActivationFunctionType.Silu
+
+P = 128
+PACK = 4
+K_PASS = P * PACK
+PASSES = K // K_PASS
+X_CHUNKS = ((512, 512), (512, 256, 256))
+HALF = S // 2
+CHUNK = 128
+CHUNKS = S // CHUNK
+
+
+def tile_picked_route2_glusilu_e_kernel(
+    tc, xT, gate, w1, w3, w2_words, w2_scales, offs, dst, out
+):
+    nc = tc.nc
+    with ExitStack() as ctx:
+        keep = ctx.enter_context(tc.tile_pool(name="keep", bufs=1))
+        psum = ctx.enter_context(tc.psum_pool(name="psum", bufs=1))
+
+        def rows_of_pass(matrix, g, cols):
+            return matrix[g * K_PASS : (g + 1) * K_PASS, cols].rearrange("(p j) c -> p j c", j=PACK)
+
+        def load(name, matrix, g, cols):
+            raw = keep.tile([P, PACK, cols.stop - cols.start], F32, name=name)
+            nc.sync.dma_start(out=raw[:], in_=rows_of_pass(matrix, g, cols))
+            return raw
+
+        def token_chunks(g):
+            widths = X_CHUNKS[g]
+            return [slice(sum(widths[:c]), sum(widths[: c + 1])) for c in range(len(widths))]
+
+        warm = keep.tile([P, 8], F32, name="warm")
+        nc.vector.memset(warm[:], 0.0)
+        nc.scalar.activation(warm[:, 4:8], warm[:, 0:4], SILU)
+
+        x_scales = keep.tile([P, T], U8, name="x_scales", align_bytes=64)
+        nc.vector.memset(x_scales[:], 0)
+        w2_plane = keep.tile([P, N], U8, name="w2_plane", align_bytes=64)
+        nc.vector.memset(w2_plane[:], 0)
+        placed = keep.tile([P, U], F32, name="placed")
+        nc.vector.memset(placed[:], 0.0)
+
+        x_raw = {}
+        picks = keep.tile([P, S // 16], U16, name="picks")
+        for g in range(PASSES):
+            for c, cols in enumerate(token_chunks(g)):
+                x_raw[g, c] = load("x_raw%d%d" % (g, c), xT, g, cols)
+            if g == 0:
+                nc.sync.dma_start(picks[:], offs)
+        w1_raw = [load("w1_raw%d" % g, w1, g, slice(0, H)) for g in range(PASSES)]
+        w3_raw0 = load("w3_raw0", w3, 0, slice(0, H))
+        w3_raw1 = [load("w3_raw1%d" % u, w3, 1, slice(u * H // 2, (u + 1) * H // 2)) for u in range(2)]
+        w2_codes = keep.tile([P, N], U32, name="w2_codes", align_bytes=64)
+        nc.sync.dma_start(
+            out=w2_codes[:].bitcast(I32), in_=w2_words[0].rearrange("p n t -> p (n t)").bitcast(I32)
+        )
+        for q in range(4):
+            nc.sync.dma_start(
+                out=w2_plane[32 * q : 32 * q + 4, :].bitcast(I32),
+                in_=w2_scales[0, 4 * q : 4 * q + 4, :].bitcast(I32),
+            )
+        gates = keep.tile([P, S], F32, name="gates")
+        nc.sync.dma_start(out=gates[:], in_=gate)
+        places = keep.tile([P, S // 16], U16, name="places")
+        nc.sync.dma_start(places[:], dst)
+
+        picked_codes = []
+        picked_scales = keep.tile([P, S], U8, name="picked_scales", align_bytes=64)
+        for g in range(PASSES):
+            x_codes = keep.tile([P, T], U32, name="x_codes%d" % g, align_bytes=64)
+            for c, cols in enumerate(token_chunks(g)):
+                width = cols.stop - cols.start
+                on_vector = width // 2 if width == 512 else 160
+                grouped = keep.tile([P, width, PACK], BF16, name="x_bf%d%d" % (g, c), align_bytes=64)
+                for copy, part in (
+                    (nc.scalar.copy, slice(on_vector, width)),
+                    (nc.vector.tensor_copy, slice(0, on_vector)),
+                ):
+                    copy(
+                        grouped[:, part, :].rearrange("p (c i) j -> p c j i", i=4),
+                        x_raw[g, c][:, :, part].rearrange("p j (c i) -> p c j i", i=4),
+                    )
+                nc.vector.quantize_mx(
+                    out=x_codes[:, cols].bitcast(FP8X4),
+                    scales=x_scales[4 * g : P, cols],
+                    in_=grouped[:].rearrange("p c j -> p (c j)"),
+                )
+            if g == PASSES - 1:
+                nc.vector.tensor_copy(picked_scales[:], x_scales[:].indirect(picks[:]))
+            codes = keep.tile([P, S], U32, name="picked_codes%d" % g, align_bytes=64)
+            nc.vector.tensor_copy(codes[:], x_codes[:].indirect(picks[:]))
+            picked_codes.append(codes)
+
+        def weight_tiles(name):
+            grouped = keep.tile([P, PACK, P, PACK], BF16, name=name + "_bf", align_bytes=64)
+            codes = keep.tile([P, H], U32, name=name + "_codes", align_bytes=64)
+            scales = keep.tile([P, H], U8, name=name + "_scales", align_bytes=64)
+            return grouped, codes, scales
+
+        def deal(tiles, raw, m0, width, shared=True):
+            shares = ((nc.scalar.copy, slice(2, 4)), (nc.vector.tensor_copy, slice(0, 2)))
+            for copy, ts in shares if shared else ((nc.vector.tensor_copy, slice(0, 4)),):
+                copy(
+                    tiles[0][:, ts, m0 : m0 + width, :].rearrange("p t m j -> p m j t"),
+                    raw[:].rearrange("p j (m t) -> p m j t", t=PACK)[:, :, :, ts],
+                )
+
+        def quantize_weight(tiles, t0, t1, m0, m1):
+            grouped, codes, scales = tiles
+            lo, hi = t0 * P + m0, (t1 - 1) * P + m1
+            nc.vector.quantize_mx(
+                out=codes[:, lo:hi].bitcast(FP8X4),
+                scales=scales[:, lo:hi],
+                in_=grouped[:].rearrange("p t m j -> p (t m j)")[:, PACK * lo : PACK * hi],
+            )
+
+        def first_layer(acc, tiles, g, t, cols):
+            nc.tensor.matmul_mx(
+                out=acc,
+                lhsT=tiles[1][:, t * P : (t + 1) * P].bitcast(FP8X4),
+                lhsT_scale=tiles[2][:, t * P : (t + 1) * P],
+                rhs=picked_codes[g][:, cols].bitcast(FP8X4),
+                rhs_scale=picked_scales[4 * g : P, cols],
+                start=(g == 0),
+                stop=(g == PASSES - 1),
+            )
+
+        w1_q = [weight_tiles("w1_%d" % g) for g in range(PASSES)]
+        w3_q = [weight_tiles("w3_%d" % g) for g in range(PASSES)]
+        a_acc = [psum.tile([P, S], F32, name="a_acc%d" % t, tag="bank%d" % t) for t in range(PACK)]
+        silu_a = [keep.tile([P, PACK, HALF], F32, name="silu_a%d" % u) for u in range(2)]
+        halves = [slice(u * HALF, (u + 1) * HALF) for u in range(2)]
+
+        def silu(t, u):
+            nc.scalar.activation(silu_a[u][:, t, :], a_acc[t][:, halves[u]], SILU)
+
+        deal(w1_q[0], w1_raw[0], 0, P)
+        for t in range(0, PACK, 2):
+            quantize_weight(w1_q[0], t, t + 2, 0, P)
+        for t in range(PACK):
+            first_layer(a_acc[t][:, halves[0]], w1_q[0], 0, t, halves[0])
+        deal(w1_q[1], w1_raw[1], 0, P)
+        for t in range(PACK):
+            quantize_weight(w1_q[1], t, t + 1, 0, P)
+            first_layer(a_acc[t][:, halves[0]], w1_q[1], 1, t, halves[0])
+        for t in range(PACK):
+            silu(t, 0)
+            for g in range(PASSES):
+                first_layer(a_acc[t][:, halves[1]], w1_q[g], g, t, halves[1])
+        deal(w3_q[0], w3_raw0, 0, P, shared=False)
+        quantize_weight(w3_q[0], 0, PACK, 0, P)
+        for u in range(2):
+            deal(w3_q[1], w3_raw1[u], u * P // 2, P // 2)
+            for t in range(PACK):
+                quantize_weight(w3_q[1], t, t + 1, u * P // 2, (u + 1) * P // 2)
+        for t in range(PACK):
+            silu(t, 1)
+
+        h_bf, h_codes, h_scales, y_sb = [], [], [], []
+
+        def multiply(c):
+            cols = slice(c * CHUNK, (c + 1) * CHUNK)
+            b_acc = psum.tile([P, PACK, CHUNK], F32, name="b_acc%d" % c, tag="bank%d" % (PACK + c))
+            for t in range(PACK):
+                for g in range(PASSES):
+                    first_layer(b_acc[:, t, :], w3_q[g], g, t, cols)
+            h = keep.tile([P, CHUNK, PACK], BF16, name="h_bf%d" % c, align_bytes=64)
+            nc.vector.tensor_tensor(
+                h[:].rearrange("p (n i) t -> p n t i", i=4),
+                b_acc[:].rearrange("p t (n i) -> p n t i", i=4),
+                silu_a[c // 2][:, :, (c % 2) * CHUNK : (c % 2 + 1) * CHUNK].rearrange("p t (n i) -> p n t i", i=4),
+                MULT,
+            )
+            h_bf.append(h)
+
+        def second_layer(c):
+            codes = keep.tile([P, CHUNK], U32, name="h_codes%d" % c, align_bytes=64)
+            scales = keep.tile([P, CHUNK], U8, name="h_scales%d" % c, align_bytes=64)
+            nc.vector.quantize_mx(
+                out=codes[:].bitcast(FP8X4), scales=scales[:], in_=h_bf[c][:].rearrange("p n t -> p (n t)")
+            )
+            y_acc = psum.tile([P, CHUNK], F32, name="y_acc%d" % c, tag="bank%d" % (PACK + c))
+            nc.tensor.matmul_mx(
+                out=y_acc[:],
+                lhsT=w2_codes[:].bitcast(FP8X4),
+                lhsT_scale=w2_plane[:],
+                rhs=codes[:].bitcast(FP8X4),
+                rhs_scale=scales[:],
+                start=True,
+                stop=True,
+            )
+            y = keep.tile([P, CHUNK], F32, name="y%d" % c)
+            nc.scalar.copy(y[:], y_acc[:])
+            y_sb.append(y)
+
+        def put_back(c):
+            cols = slice(c * CHUNK, (c + 1) * CHUNK)
+            entries = slice(c * CHUNK // 16, (c + 1) * CHUNK // 16)
+            nc.vector.tensor_tensor(placed[:].indirect(places[:, entries]), y_sb[c][:], gates[:, cols], MULT)
+
+        multiply(0)
+        for c in range(CHUNKS):
+            if c + 1 < CHUNKS:
+                multiply(c + 1)
+            second_layer(c)
+            if c > 0:
+                put_back(c - 1)
+        put_back(CHUNKS - 1)
+        nc.sync.dma_start(out=out, in_=placed[:])

@@ -20,7 +20,6 @@ PACK = 4
 K_PASS = P * PACK
 PASSES = K // K_PASS
 X_CHUNKS = ((512, 512), (512, 256, 256))
-HALF = S // 2
 CHUNK = 128
 CHUNKS = S // CHUNK
 
@@ -37,7 +36,7 @@ def tile_picked_route2_glusilu_e_kernel(
             return matrix[g * K_PASS : (g + 1) * K_PASS, cols].rearrange("(p j) c -> p j c", j=PACK)
 
         def load(name, matrix, g, cols):
-            raw = keep.tile([P, PACK, cols.stop - cols.start], F32, name=name)
+            raw = keep.tile([P, PACK, cols.stop - cols.start], F32, name=name, tag=name)
             nc.sync.dma_start(out=raw[:], in_=rows_of_pass(matrix, g, cols))
             return raw
 
@@ -108,33 +107,33 @@ def tile_picked_route2_glusilu_e_kernel(
             picked_codes.append(codes)
 
         def weight_tiles(name):
-            grouped = keep.tile([P, PACK, P, PACK], BF16, name=name + "_bf", align_bytes=64)
             codes = keep.tile([P, H], U32, name=name + "_codes", align_bytes=64)
             scales = keep.tile([P, H], U8, name=name + "_scales", align_bytes=64)
-            return grouped, codes, scales
+            return codes, scales
 
-        def deal(tiles, raw, m0, width, shared=True):
-            shares = ((nc.scalar.copy, slice(2, 4)), (nc.vector.tensor_copy, slice(0, 2)))
-            for copy, ts in shares if shared else ((nc.vector.tensor_copy, slice(0, 4)),):
+        def deal(name, raw):
+            grouped = keep.tile([P, PACK, raw.shape[2] // PACK, PACK], BF16, name=name, align_bytes=64)
+            for copy, ts in ((nc.scalar.copy, slice(2, 4)), (nc.vector.tensor_copy, slice(0, 2))):
                 copy(
-                    tiles[0][:, ts, m0 : m0 + width, :].rearrange("p t m j -> p m j t"),
+                    grouped[:, ts, :, :].rearrange("p t m j -> p m j t"),
                     raw[:].rearrange("p j (m t) -> p m j t", t=PACK)[:, :, :, ts],
                 )
+            return grouped
 
-        def quantize_weight(tiles, t0, t1, m0, m1):
-            grouped, codes, scales = tiles
-            lo, hi = t0 * P + m0, (t1 - 1) * P + m1
+        def quantize_weight(w_q, grouped, t0, t1, m0=0):
+            lo = t0 * P + m0
+            hi = lo + (t1 - t0) * grouped.shape[2]
             nc.vector.quantize_mx(
-                out=codes[:, lo:hi].bitcast(FP8X4),
-                scales=scales[:, lo:hi],
-                in_=grouped[:].rearrange("p t m j -> p (t m j)")[:, PACK * lo : PACK * hi],
+                out=w_q[0][:, lo:hi].bitcast(FP8X4),
+                scales=w_q[1][:, lo:hi],
+                in_=grouped[:, t0:t1, :, :].rearrange("p t m j -> p (t m j)"),
             )
 
         def first_layer(acc, tiles, g, t, cols):
             nc.tensor.matmul_mx(
                 out=acc,
-                lhsT=tiles[1][:, t * P : (t + 1) * P].bitcast(FP8X4),
-                lhsT_scale=tiles[2][:, t * P : (t + 1) * P],
+                lhsT=tiles[0][:, t * P : (t + 1) * P].bitcast(FP8X4),
+                lhsT_scale=tiles[1][:, t * P : (t + 1) * P],
                 rhs=picked_codes[g][:, cols].bitcast(FP8X4),
                 rhs_scale=picked_scales[4 * g : P, cols],
                 start=(g == 0),
@@ -143,50 +142,44 @@ def tile_picked_route2_glusilu_e_kernel(
 
         w1_q = [weight_tiles("w1_%d" % g) for g in range(PASSES)]
         w3_q = [weight_tiles("w3_%d" % g) for g in range(PASSES)]
-        a_acc = [psum.tile([P, S], F32, name="a_acc%d" % t, tag="bank%d" % t) for t in range(PACK)]
-        silu_a = [keep.tile([P, PACK, HALF], F32, name="silu_a%d" % u) for u in range(2)]
-        halves = [slice(u * HALF, (u + 1) * HALF) for u in range(2)]
+        silu_a = []
 
-        def silu(t, u):
-            nc.scalar.activation(silu_a[u][:, t, :], a_acc[t][:, halves[u]], SILU)
-
-        deal(w1_q[0], w1_raw[0], 0, P)
-        for t in range(0, PACK, 2):
-            quantize_weight(w1_q[0], t, t + 2, 0, P)
-        for t in range(PACK):
-            first_layer(a_acc[t][:, halves[0]], w1_q[0], 0, t, halves[0])
-        deal(w1_q[1], w1_raw[1], 0, P)
-        for t in range(PACK):
-            quantize_weight(w1_q[1], t, t + 1, 0, P)
-            first_layer(a_acc[t][:, halves[0]], w1_q[1], 1, t, halves[0])
-        for t in range(PACK):
-            silu(t, 0)
-            for g in range(PASSES):
-                first_layer(a_acc[t][:, halves[1]], w1_q[g], g, t, halves[1])
-        deal(w3_q[0], w3_raw0, 0, P, shared=False)
-        quantize_weight(w3_q[0], 0, PACK, 0, P)
-        for u in range(2):
-            deal(w3_q[1], w3_raw1[u], u * P // 2, P // 2)
+        def product(name, bank, w_q, c):
+            cols = slice(c * CHUNK, (c + 1) * CHUNK)
+            acc = psum.tile([P, PACK, CHUNK], F32, name="%s%d" % (name, c), tag="bank%d" % bank)
             for t in range(PACK):
-                quantize_weight(w3_q[1], t, t + 1, u * P // 2, (u + 1) * P // 2)
+                for g in range(PASSES):
+                    first_layer(acc[:, t, :], w_q[g], g, t, cols)
+            return acc
+
+        def silu(c, act):
+            nc.scalar.activation(act, a_acc[c][:].rearrange("p t n -> p n t"), SILU)
+            silu_a.append(act)
+
+        grouped = deal("w1_bf0", w1_raw[0])
+        for t in range(0, PACK, 2):
+            quantize_weight(w1_q[0], grouped, t, t + 2)
+        grouped = deal("w1_bf1", w1_raw[1])
         for t in range(PACK):
-            silu(t, 1)
+            quantize_weight(w1_q[1], grouped, t, t + 1)
+        a_acc = [product("a_acc", c, w1_q, c) for c in range(CHUNKS)]
+        grouped = deal("w3_bf0", w3_raw0)
+        for t in range(0, PACK, 2):
+            quantize_weight(w3_q[0], grouped, t, t + 2)
+        for u, chunks in enumerate((range(0, 1), range(1, CHUNKS))):
+            grouped = deal("w3_bf1%d" % u, w3_raw1[u])
+            for t in range(PACK):
+                quantize_weight(w3_q[1], grouped, t, t + 1, u * P // 2)
+            acts = keep.tile([P, len(chunks), CHUNK, PACK], F32, name="silu_a%d" % u, tag="w3_raw1%d" % u)
+            for i, c in enumerate(chunks):
+                silu(c, acts[:, i, :, :])
 
         h_bf, h_codes, h_scales, y_sb = [], [], [], []
 
         def multiply(c):
-            cols = slice(c * CHUNK, (c + 1) * CHUNK)
-            b_acc = psum.tile([P, PACK, CHUNK], F32, name="b_acc%d" % c, tag="bank%d" % (PACK + c))
-            for t in range(PACK):
-                for g in range(PASSES):
-                    first_layer(b_acc[:, t, :], w3_q[g], g, t, cols)
+            b_acc = product("b_acc", CHUNKS + c, w3_q, c)
             h = keep.tile([P, CHUNK, PACK], BF16, name="h_bf%d" % c, align_bytes=64)
-            nc.vector.tensor_tensor(
-                h[:].rearrange("p (n i) t -> p n t i", i=4),
-                b_acc[:].rearrange("p t (n i) -> p n t i", i=4),
-                silu_a[c // 2][:, :, (c % 2) * CHUNK : (c % 2 + 1) * CHUNK].rearrange("p t (n i) -> p n t i", i=4),
-                MULT,
-            )
+            nc.vector.tensor_tensor(h[:], b_acc[:].rearrange("p t n -> p n t"), silu_a[c], MULT)
             h_bf.append(h)
 
         def second_layer(c):
@@ -195,7 +188,7 @@ def tile_picked_route2_glusilu_e_kernel(
             nc.vector.quantize_mx(
                 out=codes[:].bitcast(FP8X4), scales=scales[:], in_=h_bf[c][:].rearrange("p n t -> p (n t)")
             )
-            y_acc = psum.tile([P, CHUNK], F32, name="y_acc%d" % c, tag="bank%d" % (PACK + c))
+            y_acc = psum.tile([P, CHUNK], F32, name="y_acc%d" % c, tag="bank%d" % (CHUNKS + c))
             nc.tensor.matmul_mx(
                 out=y_acc[:],
                 lhsT=w2_codes[:].bitcast(FP8X4),

@@ -20,6 +20,7 @@ PACK = 4
 K_PASS = P * PACK
 PASSES = K // K_PASS
 X_CHUNKS = ((512, 512), (512, 256, 256))
+X_ON_VECTOR = ((192, 192), (192, 96, 144))
 CHUNK = 128
 CHUNKS = S // CHUNK
 
@@ -43,10 +44,6 @@ def tile_picked_route2_glusilu_e_kernel(
         def token_chunks(g):
             widths = X_CHUNKS[g]
             return [slice(sum(widths[:c]), sum(widths[: c + 1])) for c in range(len(widths))]
-
-        warm = keep.tile([P, 8], F32, name="warm")
-        nc.vector.memset(warm[:], 0.0)
-        nc.scalar.activation(warm[:, 4:8], warm[:, 0:4], SILU)
 
         x_scales = keep.tile([P, T], U8, name="x_scales", align_bytes=64)
         nc.vector.memset(x_scales[:], 0)
@@ -85,7 +82,7 @@ def tile_picked_route2_glusilu_e_kernel(
             x_codes = keep.tile([P, T], U32, name="x_codes%d" % g, align_bytes=64)
             for c, cols in enumerate(token_chunks(g)):
                 width = cols.stop - cols.start
-                on_vector = width // 2 if width == 512 else 160
+                on_vector = X_ON_VECTOR[g][c]
                 grouped = keep.tile([P, width, PACK], BF16, name="x_bf%d%d" % (g, c), align_bytes=64)
                 for copy, part in (
                     (nc.scalar.copy, slice(on_vector, width)),
@@ -115,8 +112,8 @@ def tile_picked_route2_glusilu_e_kernel(
             grouped = keep.tile([P, PACK, raw.shape[2] // PACK, PACK], BF16, name=name, align_bytes=64)
             for copy, ts in ((nc.scalar.copy, slice(2, 4)), (nc.vector.tensor_copy, slice(0, 2))):
                 copy(
-                    grouped[:, ts, :, :].rearrange("p t m j -> p m j t"),
-                    raw[:].rearrange("p j (m t) -> p m j t", t=PACK)[:, :, :, ts],
+                    grouped[:, ts, :, :].rearrange("p t (m i) j -> p m j t i", i=2),
+                    raw[:].rearrange("p j (m i t) -> p m j t i", i=2, t=PACK)[:, :, :, ts, :],
                 )
             return grouped
 
@@ -166,15 +163,16 @@ def tile_picked_route2_glusilu_e_kernel(
         grouped = deal("w3_bf0", w3_raw0)
         for t in range(0, PACK, 2):
             quantize_weight(w3_q[0], grouped, t, t + 2)
-        for u, chunks in enumerate((range(0, 1), range(1, CHUNKS))):
+        for u in range(2):
             grouped = deal("w3_bf1%d" % u, w3_raw1[u])
             for t in range(PACK):
                 quantize_weight(w3_q[1], grouped, t, t + 1, u * P // 2)
-            acts = keep.tile([P, len(chunks), CHUNK, PACK], F32, name="silu_a%d" % u, tag="w3_raw1%d" % u)
-            for i, c in enumerate(chunks):
-                silu(c, acts[:, i, :, :])
+        acts = keep.tile([P, CHUNKS, CHUNK, PACK], F32, name="silu_a", tag="w3_raw11")
+        for c in range(CHUNKS):
+            silu(c, acts[:, c, :, :])
 
-        h_bf, h_codes, h_scales, y_sb = [], [], [], []
+        h_bf = []
+        y_sb = [keep.tile([P, 2 * CHUNK], F32, name="y%d" % u) for u in range(2)]
 
         def multiply(c):
             b_acc = product("b_acc", CHUNKS + c, w3_q, c)
@@ -198,21 +196,18 @@ def tile_picked_route2_glusilu_e_kernel(
                 start=True,
                 stop=True,
             )
-            y = keep.tile([P, CHUNK], F32, name="y%d" % c)
-            nc.scalar.copy(y[:], y_acc[:])
-            y_sb.append(y)
+            nc.scalar.copy(y_sb[c // 2][:, (c % 2) * CHUNK : (c % 2 + 1) * CHUNK], y_acc[:])
 
-        def put_back(c):
-            cols = slice(c * CHUNK, (c + 1) * CHUNK)
-            entries = slice(c * CHUNK // 16, (c + 1) * CHUNK // 16)
-            nc.vector.tensor_tensor(placed[:].indirect(places[:, entries]), y_sb[c][:], gates[:, cols], MULT)
+        def put_back(u):
+            cols = slice(u * S // 2, (u + 1) * S // 2)
+            entries = slice(u * S // 32, (u + 1) * S // 32)
+            nc.vector.tensor_tensor(placed[:].indirect(places[:, entries]), y_sb[u][:], gates[:, cols], MULT)
 
         multiply(0)
         for c in range(CHUNKS):
             if c + 1 < CHUNKS:
                 multiply(c + 1)
             second_layer(c)
-            if c > 0:
-                put_back(c - 1)
-        put_back(CHUNKS - 1)
+        for u in range(2):
+            put_back(u)
         nc.sync.dma_start(out=out, in_=placed[:])

@@ -19,10 +19,12 @@ P = 128
 PACK = 4
 K_PASS = P * PACK
 PASSES = K // K_PASS
-X_CHUNKS = ((512, 512), (512, 256, 256))
-X_ON_VECTOR = ((192, 192), (192, 96, 144))
+LIST_ROWS = 16
+SCALE_ROWS = 4
 CHUNK = 128
 CHUNKS = S // CHUNK
+X_LOADS = ((512, 512), (512, 256, 256))
+X_ON_VECTOR = ((192, 192), (192, 96, 144))
 
 
 def tile_picked_route2_glusilu_e_kernel(
@@ -33,17 +35,19 @@ def tile_picked_route2_glusilu_e_kernel(
         keep = ctx.enter_context(tc.tile_pool(name="keep", bufs=1))
         psum = ctx.enter_context(tc.psum_pool(name="psum", bufs=1))
 
-        def rows_of_pass(matrix, g, cols):
-            return matrix[g * K_PASS : (g + 1) * K_PASS, cols].rearrange("(p j) c -> p j c", j=PACK)
-
         def load(name, matrix, g, cols):
             raw = keep.tile([P, PACK, cols.stop - cols.start], F32, name=name, tag=name)
-            nc.sync.dma_start(out=raw[:], in_=rows_of_pass(matrix, g, cols))
+            rows = matrix[g * K_PASS : (g + 1) * K_PASS, cols]
+            nc.sync.dma_start(out=raw[:], in_=rows.rearrange("(p j) c -> p j c", j=PACK))
             return raw
 
-        def token_chunks(g):
-            widths = X_CHUNKS[g]
+        def token_ranges(g):
+            widths = X_LOADS[g]
             return [slice(sum(widths[:c]), sum(widths[: c + 1])) for c in range(len(widths))]
+
+        warm = keep.tile([P, 8], F32, name="warm")
+        nc.vector.memset(warm[:], 0.0)
+        nc.scalar.activation(warm[:, 4:8], warm[:, 0:4], SILU)
 
         x_scales = keep.tile([P, T], U8, name="x_scales", align_bytes=64)
         nc.vector.memset(x_scales[:], 0)
@@ -53,49 +57,49 @@ def tile_picked_route2_glusilu_e_kernel(
         nc.vector.memset(placed[:], 0.0)
 
         x_raw = {}
-        picks = keep.tile([P, S // 16], U16, name="picks")
+        picks = keep.tile([P, S // LIST_ROWS], U16, name="picks")
         for g in range(PASSES):
-            for c, cols in enumerate(token_chunks(g)):
+            for c, cols in enumerate(token_ranges(g)):
                 x_raw[g, c] = load("x_raw%d%d" % (g, c), xT, g, cols)
             if g == 0:
                 nc.sync.dma_start(picks[:], offs)
         w1_raw = [load("w1_raw%d" % g, w1, g, slice(0, H)) for g in range(PASSES)]
-        w3_raw0 = load("w3_raw0", w3, 0, slice(0, H))
-        w3_raw1 = [load("w3_raw1%d" % u, w3, 1, slice(u * H // 2, (u + 1) * H // 2)) for u in range(2)]
+        w3_raw_first = load("w3_raw0", w3, 0, slice(0, H))
+        w3_raw_last = [load("w3_raw1%d" % u, w3, 1, slice(u * H // 2, (u + 1) * H // 2)) for u in range(2)]
         w2_codes = keep.tile([P, N], U32, name="w2_codes", align_bytes=64)
         nc.sync.dma_start(
             out=w2_codes[:].bitcast(I32), in_=w2_words[0].rearrange("p n t -> p (n t)").bitcast(I32)
         )
-        for q in range(4):
+        for quadrant in range(P // 32):
             nc.sync.dma_start(
-                out=w2_plane[32 * q : 32 * q + 4, :].bitcast(I32),
-                in_=w2_scales[0, 4 * q : 4 * q + 4, :].bitcast(I32),
+                out=w2_plane[32 * quadrant : 32 * quadrant + SCALE_ROWS, :].bitcast(I32),
+                in_=w2_scales[0, SCALE_ROWS * quadrant : SCALE_ROWS * (quadrant + 1), :].bitcast(I32),
             )
         gates = keep.tile([P, S], F32, name="gates")
         nc.sync.dma_start(out=gates[:], in_=gate)
-        places = keep.tile([P, S // 16], U16, name="places")
+        places = keep.tile([P, S // LIST_ROWS], U16, name="places")
         nc.sync.dma_start(places[:], dst)
 
         picked_codes = []
         picked_scales = keep.tile([P, S], U8, name="picked_scales", align_bytes=64)
         for g in range(PASSES):
             x_codes = keep.tile([P, T], U32, name="x_codes%d" % g, align_bytes=64)
-            for c, cols in enumerate(token_chunks(g)):
+            for c, cols in enumerate(token_ranges(g)):
                 width = cols.stop - cols.start
                 on_vector = X_ON_VECTOR[g][c]
-                grouped = keep.tile([P, width, PACK], BF16, name="x_bf%d%d" % (g, c), align_bytes=64)
+                x_bf = keep.tile([P, width, PACK], BF16, name="x_bf%d%d" % (g, c), align_bytes=64)
                 for copy, part in (
                     (nc.scalar.copy, slice(on_vector, width)),
                     (nc.vector.tensor_copy, slice(0, on_vector)),
                 ):
                     copy(
-                        grouped[:, part, :].rearrange("p (c i) j -> p c j i", i=4),
+                        x_bf[:, part, :].rearrange("p (c i) j -> p c j i", i=4),
                         x_raw[g, c][:, :, part].rearrange("p j (c i) -> p c j i", i=4),
                     )
                 nc.vector.quantize_mx(
                     out=x_codes[:, cols].bitcast(FP8X4),
-                    scales=x_scales[4 * g : P, cols],
-                    in_=grouped[:].rearrange("p c j -> p (c j)"),
+                    scales=x_scales[SCALE_ROWS * g : P, cols],
+                    in_=x_bf[:].rearrange("p c j -> p (c j)"),
                 )
             if g == PASSES - 1:
                 nc.vector.tensor_copy(picked_scales[:], x_scales[:].indirect(picks[:]))
@@ -104,110 +108,102 @@ def tile_picked_route2_glusilu_e_kernel(
             picked_codes.append(codes)
 
         def weight_tiles(name):
-            codes = keep.tile([P, H], U32, name=name + "_codes", align_bytes=64)
+            words = keep.tile([P, H], U32, name=name + "_codes", align_bytes=64)
             scales = keep.tile([P, H], U8, name=name + "_scales", align_bytes=64)
-            return codes, scales
+            return words, scales
 
         def deal(name, raw):
-            grouped = keep.tile([P, PACK, raw.shape[2] // PACK, PACK], BF16, name=name, align_bytes=64)
+            dealt = keep.tile([P, PACK, raw.shape[2] // PACK, PACK], BF16, name=name, align_bytes=64)
             for copy, ts in ((nc.scalar.copy, slice(2, 4)), (nc.vector.tensor_copy, slice(0, 2))):
                 copy(
-                    grouped[:, ts, :, :].rearrange("p t (m i) j -> p m j t i", i=2),
+                    dealt[:, ts, :, :].rearrange("p t (m i) j -> p m j t i", i=2),
                     raw[:].rearrange("p j (m i t) -> p m j t i", i=2, t=PACK)[:, :, :, ts, :],
                 )
-            return grouped
+            return dealt
 
-        def quantize_weight(w_q, grouped, t0, t1, m0=0):
+        def quantize_weight(w_pass, dealt, t0, t1, m0=0):
+            words, scales = w_pass
             lo = t0 * P + m0
-            hi = lo + (t1 - t0) * grouped.shape[2]
+            hi = lo + (t1 - t0) * dealt.shape[2]
             nc.vector.quantize_mx(
-                out=w_q[0][:, lo:hi].bitcast(FP8X4),
-                scales=w_q[1][:, lo:hi],
-                in_=grouped[:, t0:t1, :, :].rearrange("p t m j -> p (t m j)"),
+                out=words[:, lo:hi].bitcast(FP8X4),
+                scales=scales[:, lo:hi],
+                in_=dealt[:, t0:t1, :, :].rearrange("p t m j -> p (t m j)"),
             )
 
-        def first_layer(acc, tiles, g, t, cols):
-            nc.tensor.matmul_mx(
-                out=acc,
-                lhsT=tiles[0][:, t * P : (t + 1) * P].bitcast(FP8X4),
-                lhsT_scale=tiles[1][:, t * P : (t + 1) * P],
-                rhs=picked_codes[g][:, cols].bitcast(FP8X4),
-                rhs_scale=picked_scales[4 * g : P, cols],
-                start=(g == 0),
-                stop=(g == PASSES - 1),
-            )
-
-        w1_q = [weight_tiles("w1_%d" % g) for g in range(PASSES)]
-        w3_q = [weight_tiles("w3_%d" % g) for g in range(PASSES)]
-        silu_a = []
-
-        def product(name, bank, w_q, c):
+        def first_layer(name, bank, w_q, c):
             cols = slice(c * CHUNK, (c + 1) * CHUNK)
             acc = psum.tile([P, PACK, CHUNK], F32, name="%s%d" % (name, c), tag="bank%d" % bank)
             for t in range(PACK):
                 for g in range(PASSES):
-                    first_layer(acc[:, t, :], w_q[g], g, t, cols)
+                    words, scales = w_q[g]
+                    nc.tensor.matmul_mx(
+                        out=acc[:, t, :],
+                        lhsT=words[:, t * P : (t + 1) * P].bitcast(FP8X4),
+                        lhsT_scale=scales[:, t * P : (t + 1) * P],
+                        rhs=picked_codes[g][:, cols].bitcast(FP8X4),
+                        rhs_scale=picked_scales[SCALE_ROWS * g : P, cols],
+                        start=(g == 0),
+                        stop=(g == PASSES - 1),
+                    )
             return acc
 
-        def silu(c, act):
-            nc.scalar.activation(act, a_acc[c][:].rearrange("p t n -> p n t"), SILU)
-            silu_a.append(act)
-
-        grouped = deal("w1_bf0", w1_raw[0])
+        w1_q = [weight_tiles("w1_%d" % g) for g in range(PASSES)]
+        w3_q = [weight_tiles("w3_%d" % g) for g in range(PASSES)]
+        dealt = deal("w1_bf0", w1_raw[0])
         for t in range(0, PACK, 2):
-            quantize_weight(w1_q[0], grouped, t, t + 2)
-        grouped = deal("w1_bf1", w1_raw[1])
+            quantize_weight(w1_q[0], dealt, t, t + 2)
+        dealt = deal("w1_bf1", w1_raw[1])
         for t in range(PACK):
-            quantize_weight(w1_q[1], grouped, t, t + 1)
-        a_acc = [product("a_acc", c, w1_q, c) for c in range(CHUNKS)]
-        grouped = deal("w3_bf0", w3_raw0)
+            quantize_weight(w1_q[1], dealt, t, t + 1)
+        a_acc = [first_layer("a_acc", c, w1_q, c) for c in range(CHUNKS)]
+        dealt = deal("w3_bf0", w3_raw_first)
         for t in range(0, PACK, 2):
-            quantize_weight(w3_q[0], grouped, t, t + 2)
+            quantize_weight(w3_q[0], dealt, t, t + 2)
         for u in range(2):
-            grouped = deal("w3_bf1%d" % u, w3_raw1[u])
+            dealt = deal("w3_bf1%d" % u, w3_raw_last[u])
             for t in range(PACK):
-                quantize_weight(w3_q[1], grouped, t, t + 1, u * P // 2)
-        acts = keep.tile([P, CHUNKS, CHUNK, PACK], F32, name="silu_a", tag="w3_raw11")
+                quantize_weight(w3_q[1], dealt, t, t + 1, u * P // 2)
+
+        silu_a = keep.tile([P, CHUNKS, CHUNK, PACK], F32, name="silu_a", tag="w3_raw11")
         for c in range(CHUNKS):
-            silu(c, acts[:, c, :, :])
+            nc.scalar.activation(silu_a[:, c, :, :], a_acc[c][:].rearrange("p t n -> p n t"), SILU)
 
         h_bf = []
-        y_sb = [keep.tile([P, 2 * CHUNK], F32, name="y%d" % u) for u in range(2)]
+        y_half = [keep.tile([P, S // 2], F32, name="y%d" % u) for u in range(2)]
 
-        def multiply(c):
-            b_acc = product("b_acc", CHUNKS + c, w3_q, c)
+        def make_h(c):
+            b_acc = first_layer("b_acc", CHUNKS + c, w3_q, c)
             h = keep.tile([P, CHUNK, PACK], BF16, name="h_bf%d" % c, align_bytes=64)
-            nc.vector.tensor_tensor(h[:], b_acc[:].rearrange("p t n -> p n t"), silu_a[c], MULT)
+            nc.vector.tensor_tensor(h[:], b_acc[:].rearrange("p t n -> p n t"), silu_a[:, c, :, :], MULT)
             h_bf.append(h)
 
         def second_layer(c):
-            codes = keep.tile([P, CHUNK], U32, name="h_codes%d" % c, align_bytes=64)
-            scales = keep.tile([P, CHUNK], U8, name="h_scales%d" % c, align_bytes=64)
+            h_codes = keep.tile([P, CHUNK], U32, name="h_codes%d" % c, align_bytes=64)
+            h_scales = keep.tile([P, CHUNK], U8, name="h_scales%d" % c, align_bytes=64)
             nc.vector.quantize_mx(
-                out=codes[:].bitcast(FP8X4), scales=scales[:], in_=h_bf[c][:].rearrange("p n t -> p (n t)")
+                out=h_codes[:].bitcast(FP8X4), scales=h_scales[:], in_=h_bf[c][:].rearrange("p n t -> p (n t)")
             )
             y_acc = psum.tile([P, CHUNK], F32, name="y_acc%d" % c, tag="bank%d" % (CHUNKS + c))
             nc.tensor.matmul_mx(
                 out=y_acc[:],
                 lhsT=w2_codes[:].bitcast(FP8X4),
                 lhsT_scale=w2_plane[:],
-                rhs=codes[:].bitcast(FP8X4),
-                rhs_scale=scales[:],
+                rhs=h_codes[:].bitcast(FP8X4),
+                rhs_scale=h_scales[:],
                 start=True,
                 stop=True,
             )
-            nc.scalar.copy(y_sb[c // 2][:, (c % 2) * CHUNK : (c % 2 + 1) * CHUNK], y_acc[:])
+            nc.scalar.copy(y_half[c // 2][:, (c % 2) * CHUNK : (c % 2 + 1) * CHUNK], y_acc[:])
 
-        def put_back(u):
-            cols = slice(u * S // 2, (u + 1) * S // 2)
-            entries = slice(u * S // 32, (u + 1) * S // 32)
-            nc.vector.tensor_tensor(placed[:].indirect(places[:, entries]), y_sb[u][:], gates[:, cols], MULT)
-
-        multiply(0)
+        make_h(0)
         for c in range(CHUNKS):
             if c + 1 < CHUNKS:
-                multiply(c + 1)
+                make_h(c + 1)
             second_layer(c)
+
         for u in range(2):
-            put_back(u)
+            cols = slice(u * S // 2, (u + 1) * S // 2)
+            entries = slice(cols.start // LIST_ROWS, cols.stop // LIST_ROWS)
+            nc.vector.tensor_tensor(placed[:].indirect(places[:, entries]), y_half[u][:], gates[:, cols], MULT)
         nc.sync.dma_start(out=out, in_=placed[:])

@@ -24,7 +24,7 @@ SCALE_ROWS = 4
 CHUNK = 128
 CHUNKS = S // CHUNK
 X_LOADS = ((512, 512), (512, 256, 256))
-X_ON_VECTOR = ((192, 192), (192, 96, 144))
+X_ON_VECTOR = ((320, 320), (176, 64, 128))
 
 
 def tile_picked_route2_glusilu_e_kernel(
@@ -65,7 +65,8 @@ def tile_picked_route2_glusilu_e_kernel(
                 nc.sync.dma_start(picks[:], offs)
         w1_raw = [load("w1_raw%d" % g, w1, g, slice(0, H)) for g in range(PASSES)]
         w3_raw_first = load("w3_raw0", w3, 0, slice(0, H))
-        w3_raw_last = [load("w3_raw1%d" % u, w3, 1, slice(u * H // 2, (u + 1) * H // 2)) for u in range(2)]
+        last_cols = (slice(H // 2, H), slice(H // 4, H // 2), slice(0, H // 4))
+        w3_raw_last = [load("w3_raw1%d" % u, w3, 1, cols) for u, cols in enumerate(last_cols)]
         w2_codes = keep.tile([P, N], U32, name="w2_codes", align_bytes=64)
         nc.sync.dma_start(
             out=w2_codes[:].bitcast(I32), in_=w2_words[0].rearrange("p n t -> p (n t)").bitcast(I32)
@@ -112,14 +113,24 @@ def tile_picked_route2_glusilu_e_kernel(
             scales = keep.tile([P, H], U8, name=name + "_scales", align_bytes=64)
             return words, scales
 
-        def deal(name, raw):
-            dealt = keep.tile([P, PACK, raw.shape[2] // PACK, PACK], BF16, name=name, align_bytes=64)
-            for copy, ts in ((nc.scalar.copy, slice(2, 4)), (nc.vector.tensor_copy, slice(0, 2))):
-                copy(
-                    dealt[:, ts, :, :].rearrange("p t (m i) j -> p m j t i", i=2),
-                    raw[:].rearrange("p j (m i t) -> p m j t i", i=2, t=PACK)[:, :, :, ts, :],
-                )
-            return dealt
+        def deal_part(copy, dealt, raw, ts, ms, m0):
+            copy(
+                dealt[:, ts, m0 + ms.start : m0 + ms.stop, :].rearrange("p t (m i) j -> p m j t i", i=2),
+                raw[:, :, PACK * ms.start : PACK * ms.stop].rearrange("p j (m i t) -> p m j t i", i=2, t=PACK)[
+                    :, :, :, ts, :
+                ],
+            )
+
+        def deal(dealt, raw, m0=0, on_vector=None):
+            width = raw.shape[2] // PACK
+            on_vector = on_vector or width
+            if on_vector < width:
+                deal_part(nc.scalar.copy, dealt, raw, slice(0, 2), slice(on_vector, width), m0)
+            deal_part(nc.scalar.copy, dealt, raw, slice(2, 4), slice(0, width), m0)
+            deal_part(nc.vector.tensor_copy, dealt, raw, slice(0, 2), slice(0, on_vector), m0)
+
+        def dealt_tile(name, width):
+            return keep.tile([P, PACK, width, PACK], BF16, name=name, align_bytes=64)
 
         def quantize_weight(w_pass, dealt, t0, t1, m0=0):
             words, scales = w_pass
@@ -150,22 +161,30 @@ def tile_picked_route2_glusilu_e_kernel(
 
         w1_q = [weight_tiles("w1_%d" % g) for g in range(PASSES)]
         w3_q = [weight_tiles("w3_%d" % g) for g in range(PASSES)]
-        dealt = deal("w1_bf0", w1_raw[0])
+        dealt = dealt_tile("w1_bf0", P)
+        deal(dealt, w1_raw[0], on_vector=64)
         for t in range(0, PACK, 2):
             quantize_weight(w1_q[0], dealt, t, t + 2)
-        dealt = deal("w1_bf1", w1_raw[1])
+        dealt = dealt_tile("w1_bf1", P)
+        deal(dealt, w1_raw[1])
         for t in range(PACK):
             quantize_weight(w1_q[1], dealt, t, t + 1)
         a_acc = [first_layer("a_acc", c, w1_q, c) for c in range(CHUNKS)]
-        dealt = deal("w3_bf0", w3_raw_first)
+        dealt = dealt_tile("w3_bf0", P)
+        deal(dealt, w3_raw_first)
         for t in range(0, PACK, 2):
             quantize_weight(w3_q[0], dealt, t, t + 2)
-        for u in range(2):
-            dealt = deal("w3_bf1%d" % u, w3_raw_last[u])
-            for t in range(PACK):
-                quantize_weight(w3_q[1], dealt, t, t + 1, u * P // 2)
+        dealt = dealt_tile("w3_bf1_high", P // 2)
+        deal(dealt, w3_raw_last[0])
+        for t in range(PACK):
+            quantize_weight(w3_q[1], dealt, t, t + 1, P // 2)
+        dealt = dealt_tile("w3_bf1_low", P // 2)
+        deal(dealt, w3_raw_last[1], P // 4)
+        deal(dealt, w3_raw_last[2])
+        for t in range(PACK):
+            quantize_weight(w3_q[1], dealt, t, t + 1)
 
-        silu_a = keep.tile([P, CHUNKS, CHUNK, PACK], F32, name="silu_a", tag="w3_raw11")
+        silu_a = keep.tile([P, CHUNKS, CHUNK, PACK], F32, name="silu_a", tag="w3_raw12")
         for c in range(CHUNKS):
             nc.scalar.activation(silu_a[:, c, :, :], a_acc[c][:].rearrange("p t n -> p n t"), SILU)
 

@@ -145,8 +145,9 @@ def tile_picked_route2_glusilu_e_kernel(
         def first_layer(name, bank, w_q, c):
             cols = slice(c * CHUNK, (c + 1) * CHUNK)
             acc = psum.tile([P, PACK, CHUNK], F32, name="%s%d" % (name, c), tag="bank%d" % bank)
-            for t in range(PACK):
-                for g in range(PASSES):
+            for g in range(PASSES):
+                tiles = range(PACK) if g == 0 or c == 0 else range(PACK - 1, -1, -1)
+                for t in tiles:
                     words, scales = w_q[g]
                     nc.tensor.matmul_mx(
                         out=acc[:, t, :],
@@ -154,8 +155,8 @@ def tile_picked_route2_glusilu_e_kernel(
                         lhsT_scale=scales[:, t * P : (t + 1) * P],
                         rhs=picked_codes[g][:, cols].bitcast(FP8X4),
                         rhs_scale=picked_scales[SCALE_ROWS * g : P, cols],
-                        start=(g == 0),
-                        stop=(g == PASSES - 1),
+                        start=(g == 0 and t == 0),
+                        stop=(g == PASSES - 1 and t == tiles[-1]),
                     )
             return acc
 

@@ -23,8 +23,10 @@ LIST_ROWS = 16
 SCALE_ROWS = 4
 CHUNK = 128
 CHUNKS = S // CHUNK
-X_LOADS = ((512, 512), (512, 256, 256))
-X_ON_VECTOR = ((320, 320), (176, 64, 128))
+X_LOAD = T // 2
+X_ON_VECTOR = ((320, 320), (160, 336))
+W1_ON_VECTOR = P // 2
+W3_LAST_LOADS = (slice(H // 4, H), slice(0, H // 4))
 
 
 def tile_picked_route2_glusilu_e_kernel(
@@ -41,10 +43,6 @@ def tile_picked_route2_glusilu_e_kernel(
             nc.sync.dma_start(out=raw[:], in_=rows.rearrange("(p j) c -> p j c", j=PACK))
             return raw
 
-        def token_ranges(g):
-            widths = X_LOADS[g]
-            return [slice(sum(widths[:c]), sum(widths[: c + 1])) for c in range(len(widths))]
-
         warm = keep.tile([P, 8], F32, name="warm")
         nc.vector.memset(warm[:], 0.0)
         nc.scalar.activation(warm[:, 4:8], warm[:, 0:4], SILU)
@@ -59,14 +57,13 @@ def tile_picked_route2_glusilu_e_kernel(
         x_raw = {}
         picks = keep.tile([P, S // LIST_ROWS], U16, name="picks")
         for g in range(PASSES):
-            for c, cols in enumerate(token_ranges(g)):
-                x_raw[g, c] = load("x_raw%d%d" % (g, c), xT, g, cols)
+            for c in range(T // X_LOAD):
+                x_raw[g, c] = load("x_raw%d%d" % (g, c), xT, g, slice(c * X_LOAD, (c + 1) * X_LOAD))
             if g == 0:
                 nc.sync.dma_start(picks[:], offs)
         w1_raw = [load("w1_raw%d" % g, w1, g, slice(0, H)) for g in range(PASSES)]
         w3_raw_first = load("w3_raw0", w3, 0, slice(0, H))
-        last_cols = (slice(H // 2, H), slice(H // 4, H // 2), slice(0, H // 4))
-        w3_raw_last = [load("w3_raw1%d" % u, w3, 1, cols) for u, cols in enumerate(last_cols)]
+        w3_raw_last = [load("w3_raw1%d" % u, w3, 1, cols) for u, cols in enumerate(W3_LAST_LOADS)]
         w2_codes = keep.tile([P, N], U32, name="w2_codes", align_bytes=64)
         nc.sync.dma_start(
             out=w2_codes[:].bitcast(I32), in_=w2_words[0].rearrange("p n t -> p (n t)").bitcast(I32)
@@ -81,16 +78,51 @@ def tile_picked_route2_glusilu_e_kernel(
         places = keep.tile([P, S // LIST_ROWS], U16, name="places")
         nc.sync.dma_start(places[:], dst)
 
-        picked_codes = []
-        picked_scales = keep.tile([P, S], U8, name="picked_scales", align_bytes=64)
-        for g in range(PASSES):
-            x_codes = keep.tile([P, T], U32, name="x_codes%d" % g, align_bytes=64)
-            for c, cols in enumerate(token_ranges(g)):
-                width = cols.stop - cols.start
+        def weight_tiles(name):
+            words = keep.tile([P, H], U32, name=name + "_codes", align_bytes=64)
+            scales = keep.tile([P, H], U8, name=name + "_scales", align_bytes=64)
+            return words, scales
+
+        def dealt_pairs(name, width):
+            return [
+                keep.tile([P, 2, width, PACK], BF16, name=label, tag=label, align_bytes=64)
+                for label in (name + "_front", name + "_back")
+            ]
+
+        def deal_part(copy, dealt, raw, pair, ms, m0):
+            columns = raw[:, :, PACK * ms.start : PACK * ms.stop].rearrange("p j (m i t) -> p m j t i", i=2, t=PACK)
+            copy(
+                dealt[pair][:, :, m0 + ms.start : m0 + ms.stop, :].rearrange("p t (m i) j -> p m j t i", i=2),
+                columns[:, :, :, 2 * pair : 2 * pair + 2, :],
+            )
+
+        def deal(dealt, raw, on_vector, m0=0):
+            width = raw.shape[2] // PACK
+            if on_vector < width:
+                deal_part(nc.scalar.copy, dealt, raw, 0, slice(on_vector, width), m0)
+            deal_part(nc.scalar.copy, dealt, raw, 1, slice(0, width), m0)
+            deal_part(nc.vector.tensor_copy, dealt, raw, 0, slice(0, on_vector), m0)
+
+        def quantize_weight(w_pass, dealt, tiles, m0=0):
+            words, scales = w_pass
+            rounded = dealt[tiles[0] // 2][:, tiles[0] % 2 : tiles[-1] % 2 + 1, :, :]
+            lo = tiles[0] * P + m0
+            hi = lo + len(tiles) * rounded.shape[2]
+            nc.vector.quantize_mx(
+                out=words[:, lo:hi].bitcast(FP8X4),
+                scales=scales[:, lo:hi],
+                in_=rounded.rearrange("p t m j -> p (t m j)"),
+            )
+
+        x_codes = [keep.tile([P, T], U32, name="x_codes%d" % g, align_bytes=64) for g in range(PASSES)]
+
+        def quantize_tokens(g):
+            for c in range(T // X_LOAD):
+                cols = slice(c * X_LOAD, (c + 1) * X_LOAD)
                 on_vector = X_ON_VECTOR[g][c]
-                x_bf = keep.tile([P, width, PACK], BF16, name="x_bf%d%d" % (g, c), align_bytes=64)
+                x_bf = keep.tile([P, X_LOAD, PACK], BF16, name="x_bf%d%d" % (g, c), align_bytes=64)
                 for copy, part in (
-                    (nc.scalar.copy, slice(on_vector, width)),
+                    (nc.scalar.copy, slice(on_vector, X_LOAD)),
                     (nc.vector.tensor_copy, slice(0, on_vector)),
                 ):
                     copy(
@@ -98,54 +130,36 @@ def tile_picked_route2_glusilu_e_kernel(
                         x_raw[g, c][:, :, part].rearrange("p j (c i) -> p c j i", i=4),
                     )
                 nc.vector.quantize_mx(
-                    out=x_codes[:, cols].bitcast(FP8X4),
+                    out=x_codes[g][:, cols].bitcast(FP8X4),
                     scales=x_scales[SCALE_ROWS * g : P, cols],
                     in_=x_bf[:].rearrange("p c j -> p (c j)"),
                 )
-            if g == PASSES - 1:
-                nc.vector.tensor_copy(picked_scales[:], x_scales[:].indirect(picks[:]))
-            codes = keep.tile([P, S], U32, name="picked_codes%d" % g, align_bytes=64)
-            nc.vector.tensor_copy(codes[:], x_codes[:].indirect(picks[:]))
-            picked_codes.append(codes)
 
-        def weight_tiles(name):
-            words = keep.tile([P, H], U32, name=name + "_codes", align_bytes=64)
-            scales = keep.tile([P, H], U8, name=name + "_scales", align_bytes=64)
-            return words, scales
+        def gather_words(g, tag):
+            codes = keep.tile([P, S], U32, name="picked_codes%d" % g, tag=tag, align_bytes=64)
+            nc.vector.tensor_copy(codes[:], x_codes[g][:].indirect(picks[:]))
+            return codes
 
-        def deal_part(copy, dealt, raw, ts, ms, m0):
-            copy(
-                dealt[:, ts, m0 + ms.start : m0 + ms.stop, :].rearrange("p t (m i) j -> p m j t i", i=2),
-                raw[:, :, PACK * ms.start : PACK * ms.stop].rearrange("p j (m i t) -> p m j t i", i=2, t=PACK)[
-                    :, :, :, ts, :
-                ],
-            )
+        quantize_tokens(0)
+        picked_codes = [gather_words(0, "picked_codes0")]
+        quantize_tokens(1)
+        picked_scales = keep.tile([P, S], U8, name="picked_scales", align_bytes=64)
+        nc.vector.tensor_copy(picked_scales[:], x_scales[:].indirect(picks[:]))
 
-        def deal(dealt, raw, m0=0, on_vector=None):
-            width = raw.shape[2] // PACK
-            on_vector = on_vector or width
-            if on_vector < width:
-                deal_part(nc.scalar.copy, dealt, raw, slice(0, 2), slice(on_vector, width), m0)
-            deal_part(nc.scalar.copy, dealt, raw, slice(2, 4), slice(0, width), m0)
-            deal_part(nc.vector.tensor_copy, dealt, raw, slice(0, 2), slice(0, on_vector), m0)
+        w1_q = [weight_tiles("w1_%d" % g) for g in range(PASSES)]
+        w3_q = [weight_tiles("w3_%d" % g) for g in range(PASSES)]
+        dealt = dealt_pairs("w1_bf0", P)
+        deal_part(nc.scalar.copy, dealt, w1_raw[0], 0, slice(0, P), 0)
+        deal_part(nc.scalar.copy, dealt, w1_raw[0], 1, slice(W1_ON_VECTOR, P), 0)
+        quantize_weight(w1_q[0], dealt, (0, 1))
+        deal_part(nc.vector.tensor_copy, dealt, w1_raw[0], 1, slice(0, W1_ON_VECTOR), 0)
+        picked_codes.append(gather_words(1, "w1_bf0_front"))
+        quantize_weight(w1_q[0], dealt, (2, 3))
 
-        def dealt_tile(name, width):
-            return keep.tile([P, PACK, width, PACK], BF16, name=name, align_bytes=64)
-
-        def quantize_weight(w_pass, dealt, t0, t1, m0=0):
-            words, scales = w_pass
-            lo = t0 * P + m0
-            hi = lo + (t1 - t0) * dealt.shape[2]
-            nc.vector.quantize_mx(
-                out=words[:, lo:hi].bitcast(FP8X4),
-                scales=scales[:, lo:hi],
-                in_=dealt[:, t0:t1, :, :].rearrange("p t m j -> p (t m j)"),
-            )
-
-        def first_layer(name, bank, w_q, c):
+        def first_layer(name, bank, w_q, c, passes):
             cols = slice(c * CHUNK, (c + 1) * CHUNK)
             acc = psum.tile([P, PACK, CHUNK], F32, name="%s%d" % (name, c), tag="bank%d" % bank)
-            for g in range(PASSES):
+            for g in passes:
                 tiles = range(PACK) if g == 0 or c == 0 else range(PACK - 1, -1, -1)
                 for t in tiles:
                     words, scales = w_q[g]
@@ -155,37 +169,32 @@ def tile_picked_route2_glusilu_e_kernel(
                         lhsT_scale=scales[:, t * P : (t + 1) * P],
                         rhs=picked_codes[g][:, cols].bitcast(FP8X4),
                         rhs_scale=picked_scales[SCALE_ROWS * g : P, cols],
-                        start=(g == 0 and t == 0),
-                        stop=(g == PASSES - 1 and t == tiles[-1]),
+                        start=(g == passes[0] and t == tiles[0]),
+                        stop=(g == passes[-1] and t == tiles[-1]),
                     )
             return acc
 
-        w1_q = [weight_tiles("w1_%d" % g) for g in range(PASSES)]
-        w3_q = [weight_tiles("w3_%d" % g) for g in range(PASSES)]
-        dealt = dealt_tile("w1_bf0", P)
-        deal(dealt, w1_raw[0], on_vector=64)
-        for t in range(0, PACK, 2):
-            quantize_weight(w1_q[0], dealt, t, t + 2)
-        dealt = dealt_tile("w1_bf1", P)
-        deal(dealt, w1_raw[1])
-        for t in range(PACK):
-            quantize_weight(w1_q[1], dealt, t, t + 1)
-        a_acc = [first_layer("a_acc", c, w1_q, c) for c in range(CHUNKS)]
-        dealt = dealt_tile("w3_bf0", P)
-        deal(dealt, w3_raw_first)
-        for t in range(0, PACK, 2):
-            quantize_weight(w3_q[0], dealt, t, t + 2)
-        dealt = dealt_tile("w3_bf1_high", P // 2)
-        deal(dealt, w3_raw_last[0])
-        for t in range(PACK):
-            quantize_weight(w3_q[1], dealt, t, t + 1, P // 2)
-        dealt = dealt_tile("w3_bf1_low", P // 2)
-        deal(dealt, w3_raw_last[1], P // 4)
-        deal(dealt, w3_raw_last[2])
-        for t in range(PACK):
-            quantize_weight(w3_q[1], dealt, t, t + 1)
+        dealt = dealt_pairs("w1_bf1", P)
+        deal(dealt, w1_raw[1], W1_ON_VECTOR)
+        for tiles in ((0, 1), (2, 3)):
+            quantize_weight(w1_q[1], dealt, tiles)
+        a_acc = [first_layer("a_acc", c, w1_q, c, (0, 1)) for c in range(CHUNKS)]
 
-        silu_a = keep.tile([P, CHUNKS, CHUNK, PACK], F32, name="silu_a", tag="w3_raw12")
+        dealt = dealt_pairs("w3_bf0", P)
+        deal(dealt, w3_raw_first, P)
+        for tiles in ((0, 1), (2, 3)):
+            quantize_weight(w3_q[0], dealt, tiles)
+        high = dealt_pairs("w3_bf1_high", P // 2)
+        low = dealt_pairs("w3_bf1_low", P // 2)
+        deal(high, w3_raw_last[0][:, :, H // 4 :], P // 2)
+        deal(low, w3_raw_last[0][:, :, : H // 4], P // 4, P // 4)
+        for t in range(PACK):
+            quantize_weight(w3_q[1], high, (t,), P // 2)
+        deal(low, w3_raw_last[1], P // 4)
+        for t in range(PACK):
+            quantize_weight(w3_q[1], low, (t,))
+
+        silu_a = keep.tile([P, CHUNKS, CHUNK, PACK], F32, name="silu_a", tag="w3_raw11")
         for c in range(CHUNKS):
             nc.scalar.activation(silu_a[:, c, :, :], a_acc[c][:].rearrange("p t n -> p n t"), SILU)
 
@@ -193,7 +202,7 @@ def tile_picked_route2_glusilu_e_kernel(
         y_half = [keep.tile([P, S // 2], F32, name="y%d" % u) for u in range(2)]
 
         def make_h(c):
-            b_acc = first_layer("b_acc", CHUNKS + c, w3_q, c)
+            b_acc = first_layer("b_acc", CHUNKS + c, w3_q, c, (0, 1) if c < CHUNKS // 2 else (1, 0))
             h = keep.tile([P, CHUNK, PACK], BF16, name="h_bf%d" % c, align_bytes=64)
             nc.vector.tensor_tensor(h[:], b_acc[:].rearrange("p t n -> p n t"), silu_a[:, c, :, :], MULT)
             h_bf.append(h)

@@ -24,7 +24,8 @@ SCALE_ROWS = 4
 CHUNK = 128
 CHUNKS = S // CHUNK
 X_LOAD = T // 2
-X_ON_VECTOR = ((320, 320), (160, 336))
+X_ON_VECTOR = ((704, 544), (128, 240))
+DUOS = 2
 W1_ON_VECTOR = P // 2
 W3_LAST_LOADS = (slice(H // 4, H), slice(0, H // 4))
 
@@ -47,20 +48,20 @@ def tile_picked_route2_glusilu_e_kernel(
         nc.vector.memset(warm[:], 0.0)
         nc.scalar.activation(warm[:, 4:8], warm[:, 0:4], SILU)
 
-        x_scales = keep.tile([P, T], U8, name="x_scales", align_bytes=64)
-        nc.vector.memset(x_scales[:], 0)
         w2_plane = keep.tile([P, N], U8, name="w2_plane", align_bytes=64)
         nc.vector.memset(w2_plane[:], 0)
         placed = keep.tile([P, U], F32, name="placed")
         nc.vector.memset(placed[:], 0.0)
 
-        x_raw = {}
+        x_rows = {}
         picks = keep.tile([P, S // LIST_ROWS], U16, name="picks")
         for g in range(PASSES):
-            for c in range(T // X_LOAD):
-                x_raw[g, c] = load("x_raw%d%d" % (g, c), xT, g, slice(c * X_LOAD, (c + 1) * X_LOAD))
-            if g == 0:
-                nc.sync.dma_start(picks[:], offs)
+            rows = xT[g * K_PASS : (g + 1) * K_PASS, :].rearrange("(p j) c -> p j c", j=PACK)
+            for u in range(2):
+                x_rows[g, u] = keep.tile([P, 2, T], F32, name="x_rows%d%d" % (g, u))
+                nc.sync.dma_start(out=x_rows[g, u][:], in_=rows[:, 2 * u : 2 * u + 2, :])
+                if (g, u) == (0, 0):
+                    nc.sync.dma_start(picks[:], offs)
         w1_raw = [load("w1_raw%d" % g, w1, g, slice(0, H)) for g in range(PASSES)]
         w3_raw_first = load("w3_raw0", w3, 0, slice(0, H))
         w3_raw_last = [load("w3_raw1%d" % u, w3, 1, cols) for u, cols in enumerate(W3_LAST_LOADS)]
@@ -114,47 +115,41 @@ def tile_picked_route2_glusilu_e_kernel(
                 in_=rounded.rearrange("p t m j -> p (t m j)"),
             )
 
-        x_codes = [keep.tile([P, T], U32, name="x_codes%d" % g, align_bytes=64) for g in range(PASSES)]
-
-        def quantize_tokens(g):
-            for c in range(T // X_LOAD):
-                cols = slice(c * X_LOAD, (c + 1) * X_LOAD)
-                on_vector = X_ON_VECTOR[g][c]
-                x_bf = keep.tile([P, X_LOAD, PACK], BF16, name="x_bf%d%d" % (g, c), align_bytes=64)
+        picked_codes = []
+        picked_scales = []
+        for g in range(PASSES):
+            picked_duos = keep.tile([P, DUOS, S], U32, name="picked_duos%d" % g)
+            for u in range(DUOS):
+                duos = keep.tile([P, T, 2], BF16, name="duos%d%d" % (g, u))
+                on_vector = X_ON_VECTOR[g][u]
                 for copy, part in (
-                    (nc.scalar.copy, slice(on_vector, X_LOAD)),
+                    (nc.scalar.copy, slice(on_vector, T)),
                     (nc.vector.tensor_copy, slice(0, on_vector)),
                 ):
                     copy(
-                        x_bf[:, part, :].rearrange("p (c i) j -> p c j i", i=4),
-                        x_raw[g, c][:, :, part].rearrange("p j (c i) -> p c j i", i=4),
+                        duos[:, part, :].rearrange("p (c i) e -> p c e i", i=4),
+                        x_rows[g, u][:, :, part].rearrange("p e (c i) -> p c e i", i=4),
                     )
-                nc.vector.quantize_mx(
-                    out=x_codes[g][:, cols].bitcast(FP8X4),
-                    scales=x_scales[SCALE_ROWS * g : P, cols],
-                    in_=x_bf[:].rearrange("p c j -> p (c j)"),
-                )
-
-        def gather_words(g, tag):
-            codes = keep.tile([P, S], U32, name="picked_codes%d" % g, tag=tag, align_bytes=64)
-            nc.vector.tensor_copy(codes[:], x_codes[g][:].indirect(picks[:]))
-            return codes
-
-        quantize_tokens(0)
-        picked_codes = [gather_words(0, "picked_codes0")]
-        quantize_tokens(1)
-        picked_scales = keep.tile([P, S], U8, name="picked_scales", align_bytes=64)
-        nc.vector.tensor_copy(picked_scales[:], x_scales[:].indirect(picks[:]))
+                window = duos[:].rearrange("p c e -> p (c e)").bitcast(U32)
+                nc.vector.tensor_copy(picked_duos[:, u, :], window.indirect(picks[:]))
+            picked = keep.tile([P, S * PACK], BF16, name="picked%d" % g, align_bytes=64)
+            nc.vector.tensor_copy(
+                picked[:].bitcast(I32).rearrange("p (s u) -> p s u", u=DUOS),
+                picked_duos[:].bitcast(I32).rearrange("p u s -> p s u"),
+            )
+            codes = keep.tile([P, S], U32, name="picked_codes%d" % g, align_bytes=64)
+            scales = keep.tile([P, S], U8, name="picked_scales%d" % g, align_bytes=64)
+            nc.vector.quantize_mx(out=codes[:].bitcast(FP8X4), scales=scales[:], in_=picked[:])
+            picked_codes.append(codes)
+            picked_scales.append(scales)
 
         w1_q = [weight_tiles("w1_%d" % g) for g in range(PASSES)]
         w3_q = [weight_tiles("w3_%d" % g) for g in range(PASSES)]
         dealt = dealt_pairs("w1_bf0", P)
         deal_part(nc.scalar.copy, dealt, w1_raw[0], 0, slice(0, P), 0)
-        deal_part(nc.scalar.copy, dealt, w1_raw[0], 1, slice(W1_ON_VECTOR, P), 0)
-        quantize_weight(w1_q[0], dealt, (0, 1))
-        deal_part(nc.vector.tensor_copy, dealt, w1_raw[0], 1, slice(0, W1_ON_VECTOR), 0)
-        picked_codes.append(gather_words(1, "w1_bf0_front"))
-        quantize_weight(w1_q[0], dealt, (2, 3))
+        deal_part(nc.scalar.copy, dealt, w1_raw[0], 1, slice(0, P), 0)
+        for tiles in ((0, 1), (2, 3)):
+            quantize_weight(w1_q[0], dealt, tiles)
 
         def first_layer(name, bank, w_q, c, passes):
             cols = slice(c * CHUNK, (c + 1) * CHUNK)
@@ -168,7 +163,7 @@ def tile_picked_route2_glusilu_e_kernel(
                         lhsT=words[:, t * P : (t + 1) * P].bitcast(FP8X4),
                         lhsT_scale=scales[:, t * P : (t + 1) * P],
                         rhs=picked_codes[g][:, cols].bitcast(FP8X4),
-                        rhs_scale=picked_scales[SCALE_ROWS * g : P, cols],
+                        rhs_scale=picked_scales[g][:, cols],
                         start=(g == passes[0] and t == tiles[0]),
                         stop=(g == passes[-1] and t == tiles[-1]),
                     )
@@ -198,41 +193,53 @@ def tile_picked_route2_glusilu_e_kernel(
         for c in range(CHUNKS):
             nc.scalar.activation(silu_a[:, c, :, :], a_acc[c][:].rearrange("p t n -> p n t"), SILU)
 
-        h_bf = []
-        y_half = [keep.tile([P, S // 2], F32, name="y%d" % u) for u in range(2)]
+        h_bf = keep.tile([P, S, PACK], BF16, name="h_bf", align_bytes=64)
+        h_codes = keep.tile([P, S], U32, name="h_codes", align_bytes=64)
+        h_scales = keep.tile([P, S], U8, name="h_scales", align_bytes=64)
+        y = keep.tile([P, S], F32, name="y")
+
+        def entries_of(chunks):
+            return slice(chunks[0] * CHUNK, (chunks[-1] + 1) * CHUNK)
 
         def make_h(c):
             b_acc = first_layer("b_acc", CHUNKS + c, w3_q, c, (0, 1) if c < CHUNKS // 2 else (1, 0))
-            h = keep.tile([P, CHUNK, PACK], BF16, name="h_bf%d" % c, align_bytes=64)
-            nc.vector.tensor_tensor(h[:], b_acc[:].rearrange("p t n -> p n t"), silu_a[:, c, :, :], MULT)
-            h_bf.append(h)
-
-        def second_layer(c):
-            h_codes = keep.tile([P, CHUNK], U32, name="h_codes%d" % c, align_bytes=64)
-            h_scales = keep.tile([P, CHUNK], U8, name="h_scales%d" % c, align_bytes=64)
-            nc.vector.quantize_mx(
-                out=h_codes[:].bitcast(FP8X4), scales=h_scales[:], in_=h_bf[c][:].rearrange("p n t -> p (n t)")
+            nc.vector.tensor_tensor(
+                h_bf[:, entries_of((c,)), :], b_acc[:].rearrange("p t n -> p n t"), silu_a[:, c, :, :], MULT
             )
-            y_acc = psum.tile([P, CHUNK], F32, name="y_acc%d" % c, tag="bank%d" % (CHUNKS + c))
+
+        def second_layer(chunks):
+            cols = entries_of(chunks)
+            nc.vector.quantize_mx(
+                out=h_codes[:, cols].bitcast(FP8X4),
+                scales=h_scales[:, cols],
+                in_=h_bf[:, cols, :].rearrange("p n t -> p (n t)"),
+            )
+            y_acc = psum.tile(
+                [P, len(chunks) * CHUNK], F32, name="y_acc%d" % chunks[0], tag="bank%d" % (CHUNKS + chunks[0])
+            )
             nc.tensor.matmul_mx(
                 out=y_acc[:],
                 lhsT=w2_codes[:].bitcast(FP8X4),
                 lhsT_scale=w2_plane[:],
-                rhs=h_codes[:].bitcast(FP8X4),
-                rhs_scale=h_scales[:],
+                rhs=h_codes[:, cols].bitcast(FP8X4),
+                rhs_scale=h_scales[:, cols],
                 start=True,
                 stop=True,
             )
-            nc.scalar.copy(y_half[c // 2][:, (c % 2) * CHUNK : (c % 2 + 1) * CHUNK], y_acc[:])
+            nc.scalar.copy(y[:, cols], y_acc[:])
+
+        def scatter(chunks):
+            cols = entries_of(chunks)
+            entries = slice(cols.start // LIST_ROWS, cols.stop // LIST_ROWS)
+            nc.vector.tensor_tensor(placed[:].indirect(places[:, entries]), y[:, cols], gates[:, cols], MULT)
 
         make_h(0)
-        for c in range(CHUNKS):
-            if c + 1 < CHUNKS:
-                make_h(c + 1)
-            second_layer(c)
-
-        for u in range(2):
-            cols = slice(u * S // 2, (u + 1) * S // 2)
-            entries = slice(cols.start // LIST_ROWS, cols.stop // LIST_ROWS)
-            nc.vector.tensor_tensor(placed[:].indirect(places[:, entries]), y_half[u][:], gates[:, cols], MULT)
+        make_h(1)
+        second_layer((0,))
+        make_h(2)
+        make_h(3)
+        second_layer((1, 2))
+        second_layer((3,))
+        scatter((0,))
+        scatter((1, 2, 3))
         nc.sync.dma_start(out=out, in_=placed[:])

@@ -14,6 +14,7 @@ U8 = mybir.dt.uint8
 FP8X4 = mybir.dt.float8_e4m3fn_x4
 MULT = mybir.AluOpType.mult
 SILU = mybir.ActivationFunctionType.Silu
+COPY = mybir.ActivationFunctionType.Copy
 
 P = 128
 PACK = 4
@@ -23,11 +24,8 @@ LIST_ROWS = 16
 SCALE_ROWS = 4
 CHUNK = 128
 CHUNKS = S // CHUNK
-X_LOAD = T // 2
-X_ON_VECTOR = ((704, 544), (128, 240))
-DUOS = 2
-W1_ON_VECTOR = P // 2
-W3_LAST_LOADS = (slice(H // 4, H), slice(0, H // 4))
+WEAVE_ON_VECTOR = (384, 352)
+BACK_ON_VECTOR = 32
 
 
 def tile_picked_route2_glusilu_e_kernel(
@@ -38,11 +36,15 @@ def tile_picked_route2_glusilu_e_kernel(
         keep = ctx.enter_context(tc.tile_pool(name="keep", bufs=1))
         psum = ctx.enter_context(tc.psum_pool(name="psum", bufs=1))
 
-        def load(name, matrix, g, cols):
-            raw = keep.tile([P, PACK, cols.stop - cols.start], F32, name=name, tag=name)
-            rows = matrix[g * K_PASS : (g + 1) * K_PASS, cols]
-            nc.sync.dma_start(out=raw[:], in_=rows.rearrange("(p j) c -> p j c", j=PACK))
-            return raw
+        def pass_rows(matrix, g):
+            return matrix[g * K_PASS : (g + 1) * K_PASS, :].rearrange("(p j) c -> p j c", j=PACK)
+
+        def load_weight(name, matrix, g, cuts):
+            raw = keep.tile([P, PACK * H], F32, name=name, tag=name)
+            run = pass_rows(matrix, g).rearrange("p j c -> p (j c)")
+            for lo, hi in zip(cuts[:-1], cuts[1:]):
+                nc.sync.dma_start(out=raw[:, lo:hi], in_=run[:, lo:hi])
+            return raw[:].rearrange("p (j c) -> p j c", j=PACK)
 
         warm = keep.tile([P, 8], F32, name="warm")
         nc.vector.memset(warm[:], 0.0)
@@ -56,53 +58,47 @@ def tile_picked_route2_glusilu_e_kernel(
         x_rows = {}
         picks = keep.tile([P, S // LIST_ROWS], U16, name="picks")
         for g in range(PASSES):
-            rows = xT[g * K_PASS : (g + 1) * K_PASS, :].rearrange("(p j) c -> p j c", j=PACK)
             for u in range(2):
-                x_rows[g, u] = keep.tile([P, 2, T], F32, name="x_rows%d%d" % (g, u))
-                nc.sync.dma_start(out=x_rows[g, u][:], in_=rows[:, 2 * u : 2 * u + 2, :])
+                label = "x_rows%d%d" % (g, u)
+                x_rows[g, u] = keep.tile([P, 2, T], F32, name=label, tag=label, align_bytes=64)
+                nc.sync.dma_start(out=x_rows[g, u][:], in_=pass_rows(xT, g)[:, 2 * u : 2 * u + 2, :])
                 if (g, u) == (0, 0):
                     nc.sync.dma_start(picks[:], offs)
-        w1_raw = [load("w1_raw%d" % g, w1, g, slice(0, H)) for g in range(PASSES)]
-        w3_raw_first = load("w3_raw0", w3, 0, slice(0, H))
-        w3_raw_last = [load("w3_raw1%d" % u, w3, 1, cols) for u, cols in enumerate(W3_LAST_LOADS)]
+        whole = (0, PACK * H)
+        w1_raw = [load_weight("w1_raw%d" % g, w1, g, whole) for g in range(PASSES)]
+        w3_raw_first = load_weight("w3_raw0", w3, 0, whole)
+        w3_raw_last = load_weight("w3_raw1", w3, 1, (0, PACK * H - H // 2, PACK * H))
         w2_codes = keep.tile([P, N], U32, name="w2_codes", align_bytes=64)
         nc.sync.dma_start(
             out=w2_codes[:].bitcast(I32), in_=w2_words[0].rearrange("p n t -> p (n t)").bitcast(I32)
         )
-        for quadrant in range(P // 32):
-            nc.sync.dma_start(
-                out=w2_plane[32 * quadrant : 32 * quadrant + SCALE_ROWS, :].bitcast(I32),
-                in_=w2_scales[0, SCALE_ROWS * quadrant : SCALE_ROWS * (quadrant + 1), :].bitcast(I32),
-            )
         gates = keep.tile([P, S], F32, name="gates")
         nc.sync.dma_start(out=gates[:], in_=gate)
         places = keep.tile([P, S // LIST_ROWS], U16, name="places")
         nc.sync.dma_start(places[:], dst)
+        for quadrant in range(P // 32):
+            nc.gpsimd.dma_start(
+                out=w2_plane[32 * quadrant : 32 * quadrant + SCALE_ROWS, :].bitcast(I32),
+                in_=w2_scales[0, SCALE_ROWS * quadrant : SCALE_ROWS * (quadrant + 1), :].bitcast(I32),
+            )
 
         def weight_tiles(name):
             words = keep.tile([P, H], U32, name=name + "_codes", align_bytes=64)
             scales = keep.tile([P, H], U8, name=name + "_scales", align_bytes=64)
             return words, scales
 
-        def dealt_pairs(name, width):
+        def dealt_pairs(name, width, front="front", back="back"):
             return [
-                keep.tile([P, 2, width, PACK], BF16, name=label, tag=label, align_bytes=64)
-                for label in (name + "_front", name + "_back")
+                keep.tile([P, 2, width, PACK], BF16, name=name + side, tag=place, align_bytes=64)
+                for side, place in (("_front", front), ("_back", back))
             ]
 
-        def deal_part(copy, dealt, raw, pair, ms, m0):
+        def deal(copy, dealt, raw, pair, ms, m0=0):
             columns = raw[:, :, PACK * ms.start : PACK * ms.stop].rearrange("p j (m i t) -> p m j t i", i=2, t=PACK)
             copy(
-                dealt[pair][:, :, m0 + ms.start : m0 + ms.stop, :].rearrange("p t (m i) j -> p m j t i", i=2),
+                dealt[pair][:, :, ms.start - m0 : ms.stop - m0, :].rearrange("p t (m i) j -> p m j t i", i=2),
                 columns[:, :, :, 2 * pair : 2 * pair + 2, :],
             )
-
-        def deal(dealt, raw, on_vector, m0=0):
-            width = raw.shape[2] // PACK
-            if on_vector < width:
-                deal_part(nc.scalar.copy, dealt, raw, 0, slice(on_vector, width), m0)
-            deal_part(nc.scalar.copy, dealt, raw, 1, slice(0, width), m0)
-            deal_part(nc.vector.tensor_copy, dealt, raw, 0, slice(0, on_vector), m0)
 
         def quantize_weight(w_pass, dealt, tiles, m0=0):
             words, scales = w_pass
@@ -115,43 +111,53 @@ def tile_picked_route2_glusilu_e_kernel(
                 in_=rounded.rearrange("p t m j -> p (t m j)"),
             )
 
+        planes = [keep.tile([P, PACK, S], F32, name="planes%d" % g) for g in range(PASSES)]
+        picked = [keep.tile([P, S, PACK], BF16, name="picked%d" % g, align_bytes=64) for g in range(PASSES)]
         picked_codes = []
         picked_scales = []
-        for g in range(PASSES):
-            picked_duos = keep.tile([P, DUOS, S], U32, name="picked_duos%d" % g)
-            for u in range(DUOS):
-                duos = keep.tile([P, T, 2], BF16, name="duos%d%d" % (g, u))
-                on_vector = X_ON_VECTOR[g][u]
-                for copy, part in (
-                    (nc.scalar.copy, slice(on_vector, T)),
-                    (nc.vector.tensor_copy, slice(0, on_vector)),
-                ):
-                    copy(
-                        duos[:, part, :].rearrange("p (c i) e -> p c e i", i=4),
-                        x_rows[g, u][:, :, part].rearrange("p e (c i) -> p c e i", i=4),
-                    )
-                window = duos[:].rearrange("p c e -> p (c e)").bitcast(U32)
-                nc.vector.tensor_copy(picked_duos[:, u, :], window.indirect(picks[:]))
-            picked = keep.tile([P, S * PACK], BF16, name="picked%d" % g, align_bytes=64)
-            nc.vector.tensor_copy(
-                picked[:].bitcast(I32).rearrange("p (s u) -> p s u", u=DUOS),
-                picked_duos[:].bitcast(I32).rearrange("p u s -> p s u"),
-            )
-            codes = keep.tile([P, S], U32, name="picked_codes%d" % g, align_bytes=64)
+
+        def gather(g, u):
+            nc.scalar.activation(planes[g][:, 2 * u, :], x_rows[g, u][:, 0, :].indirect(picks[:]), COPY)
+            nc.vector.tensor_copy(planes[g][:, 2 * u + 1, :], x_rows[g, u][:, 1, :].indirect(picks[:]))
+
+        def weave(g):
+            on_vector = WEAVE_ON_VECTOR[g]
+            for copy, part in (
+                (nc.scalar.copy, slice(on_vector, S)),
+                (nc.vector.tensor_copy, slice(0, on_vector)),
+            ):
+                copy(
+                    picked[g][:, part, :].rearrange("p (c i) j -> p c j i", i=4),
+                    planes[g][:, :, part].rearrange("p j (c i) -> p c j i", i=4),
+                )
+
+        def quantize_tokens(g, place):
+            codes = keep.tile([P, S], U32, name="picked_codes%d" % g, tag=place, align_bytes=64)
             scales = keep.tile([P, S], U8, name="picked_scales%d" % g, align_bytes=64)
-            nc.vector.quantize_mx(out=codes[:].bitcast(FP8X4), scales=scales[:], in_=picked[:])
+            nc.vector.quantize_mx(
+                out=codes[:].bitcast(FP8X4), scales=scales[:], in_=picked[g][:].rearrange("p s j -> p (s j)")
+            )
             picked_codes.append(codes)
             picked_scales.append(scales)
 
+        gather(0, 0)
+        gather(0, 1)
+        weave(0)
+        gather(1, 0)
+        quantize_tokens(0, "x_rows10")
+        gather(1, 1)
+        weave(1)
+        w1_dealt = dealt_pairs("w1_bf0", P)
+        deal(nc.scalar.copy, w1_dealt, w1_raw[0], 1, slice(0, P))
+        deal(nc.vector.tensor_copy, w1_dealt, w1_raw[0], 0, slice(0, P))
+        quantize_tokens(1, "picked_codes1")
+
         w1_q = [weight_tiles("w1_%d" % g) for g in range(PASSES)]
         w3_q = [weight_tiles("w3_%d" % g) for g in range(PASSES)]
-        dealt = dealt_pairs("w1_bf0", P)
-        deal_part(nc.scalar.copy, dealt, w1_raw[0], 0, slice(0, P), 0)
-        deal_part(nc.scalar.copy, dealt, w1_raw[0], 1, slice(0, P), 0)
         for tiles in ((0, 1), (2, 3)):
-            quantize_weight(w1_q[0], dealt, tiles)
+            quantize_weight(w1_q[0], w1_dealt, tiles)
 
-        def first_layer(name, bank, w_q, c, passes):
+        def first_layer(name, bank, w_q, c, passes=(0, 1)):
             cols = slice(c * CHUNK, (c + 1) * CHUNK)
             acc = psum.tile([P, PACK, CHUNK], F32, name="%s%d" % (name, c), tag="bank%d" % bank)
             for g in passes:
@@ -169,56 +175,72 @@ def tile_picked_route2_glusilu_e_kernel(
                     )
             return acc
 
-        dealt = dealt_pairs("w1_bf1", P)
-        deal(dealt, w1_raw[1], W1_ON_VECTOR)
+        dealt = dealt_pairs("w1_bf1", P, back="other_back")
+        deal(nc.scalar.copy, dealt, w1_raw[1], 1, slice(BACK_ON_VECTOR, P))
+        deal(nc.vector.tensor_copy, dealt, w1_raw[1], 0, slice(0, P))
+        deal(nc.vector.tensor_copy, dealt, w1_raw[1], 1, slice(0, BACK_ON_VECTOR))
         for tiles in ((0, 1), (2, 3)):
             quantize_weight(w1_q[1], dealt, tiles)
-        a_acc = [first_layer("a_acc", c, w1_q, c, (0, 1)) for c in range(CHUNKS)]
+        a_acc = [first_layer("a_acc", c, w1_q, c, (0, 1) if c < CHUNKS // 2 else (1, 0)) for c in range(CHUNKS)]
+
+        silu_a = []
+
+        def silu(c):
+            nc.scalar.activation(silu_a[c], a_acc[c][:].rearrange("p t n -> p n t"), SILU)
 
         dealt = dealt_pairs("w3_bf0", P)
-        deal(dealt, w3_raw_first, P)
+        deal(nc.scalar.copy, dealt, w3_raw_first, 1, slice(BACK_ON_VECTOR, P))
+        deal(nc.vector.tensor_copy, dealt, w3_raw_first, 0, slice(0, P))
+        deal(nc.vector.tensor_copy, dealt, w3_raw_first, 1, slice(0, BACK_ON_VECTOR))
         for tiles in ((0, 1), (2, 3)):
             quantize_weight(w3_q[0], dealt, tiles)
-        high = dealt_pairs("w3_bf1_high", P // 2)
-        low = dealt_pairs("w3_bf1_low", P // 2)
-        deal(high, w3_raw_last[0][:, :, H // 4 :], P // 2)
-        deal(low, w3_raw_last[0][:, :, : H // 4], P // 4, P // 4)
-        for t in range(PACK):
-            quantize_weight(w3_q[1], high, (t,), P // 2)
-        deal(low, w3_raw_last[1], P // 4)
-        for t in range(PACK):
-            quantize_weight(w3_q[1], low, (t,))
-
-        silu_a = keep.tile([P, CHUNKS, CHUNK, PACK], F32, name="silu_a", tag="w3_raw11")
-        for c in range(CHUNKS):
-            nc.scalar.activation(silu_a[:, c, :, :], a_acc[c][:].rearrange("p t n -> p n t"), SILU)
+        silu_first = keep.tile([P, CHUNK, PACK], F32, name="silu_first", tag="w3_raw0")
+        silu_a.append(silu_first[:])
+        silu(0)
+        dealt = dealt_pairs("w3_bf1", P, back="other_back")
+        middle = P // 2
+        deal(nc.scalar.copy, dealt, w3_raw_last, 1, slice(0, middle))
+        deal(nc.vector.tensor_copy, dealt, w3_raw_last, 0, slice(0, middle))
+        deal(nc.scalar.copy, dealt, w3_raw_last, 1, slice(middle + BACK_ON_VECTOR, P))
+        deal(nc.vector.tensor_copy, dealt, w3_raw_last, 0, slice(middle, P))
+        deal(nc.vector.tensor_copy, dealt, w3_raw_last, 1, slice(middle, middle + BACK_ON_VECTOR))
+        for tiles in ((0, 1), (2, 3)):
+            quantize_weight(w3_q[1], dealt, tiles)
+        silu_rest = keep.tile([P, CHUNKS - 1, CHUNK, PACK], F32, name="silu_rest", tag="w3_raw1")
+        for c in range(1, CHUNKS):
+            silu_a.append(silu_rest[:, c - 1, :, :])
+            silu(c)
 
         h_bf = keep.tile([P, S, PACK], BF16, name="h_bf", align_bytes=64)
         h_codes = keep.tile([P, S], U32, name="h_codes", align_bytes=64)
         h_scales = keep.tile([P, S], U8, name="h_scales", align_bytes=64)
-        y = keep.tile([P, S], F32, name="y")
+        gated = [keep.tile([P, CHUNK], F32, name="gated%d" % c) for c in range(CHUNKS)]
+        y_acc = {}
 
-        def entries_of(chunks):
-            return slice(chunks[0] * CHUNK, (chunks[-1] + 1) * CHUNK)
+        def entries_of(c):
+            return slice(c * CHUNK, (c + 1) * CHUNK)
 
         def make_h(c):
             b_acc = first_layer("b_acc", CHUNKS + c, w3_q, c, (0, 1) if c < CHUNKS // 2 else (1, 0))
-            nc.vector.tensor_tensor(
-                h_bf[:, entries_of((c,)), :], b_acc[:].rearrange("p t n -> p n t"), silu_a[:, c, :, :], MULT
-            )
+            width = CHUNK if c == 0 else CHUNK // 2
+            for lo in range(0, CHUNK, width):
+                nc.vector.tensor_tensor(
+                    h_bf[:, c * CHUNK + lo : c * CHUNK + lo + width, :],
+                    b_acc[:, :, lo : lo + width].rearrange("p t n -> p n t"),
+                    silu_a[c][:, lo : lo + width, :],
+                    MULT,
+                )
 
-        def second_layer(chunks):
-            cols = entries_of(chunks)
+        def second_layer(c):
+            cols = entries_of(c)
             nc.vector.quantize_mx(
                 out=h_codes[:, cols].bitcast(FP8X4),
                 scales=h_scales[:, cols],
                 in_=h_bf[:, cols, :].rearrange("p n t -> p (n t)"),
             )
-            y_acc = psum.tile(
-                [P, len(chunks) * CHUNK], F32, name="y_acc%d" % chunks[0], tag="bank%d" % (CHUNKS + chunks[0])
-            )
+            y_acc[c] = psum.tile([P, CHUNK], F32, name="y_acc%d" % c, tag="bank%d" % c)
             nc.tensor.matmul_mx(
-                out=y_acc[:],
+                out=y_acc[c][:],
                 lhsT=w2_codes[:].bitcast(FP8X4),
                 lhsT_scale=w2_plane[:],
                 rhs=h_codes[:, cols].bitcast(FP8X4),
@@ -226,20 +248,17 @@ def tile_picked_route2_glusilu_e_kernel(
                 start=True,
                 stop=True,
             )
-            nc.scalar.copy(y[:, cols], y_acc[:])
 
-        def scatter(chunks):
-            cols = entries_of(chunks)
+        def place(c):
+            cols = entries_of(c)
+            nc.vector.tensor_tensor(gated[c][:], y_acc[c][:], gates[:, cols], MULT)
             entries = slice(cols.start // LIST_ROWS, cols.stop // LIST_ROWS)
-            nc.vector.tensor_tensor(placed[:].indirect(places[:, entries]), y[:, cols], gates[:, cols], MULT)
+            nc.scalar.activation(placed[:].indirect(places[:, entries]), gated[c][:], COPY)
 
         make_h(0)
-        make_h(1)
-        second_layer((0,))
-        make_h(2)
-        make_h(3)
-        second_layer((1, 2))
-        second_layer((3,))
-        scatter((0,))
-        scatter((1, 2, 3))
+        for c in range(CHUNKS):
+            second_layer(c)
+            if c + 1 < CHUNKS:
+                make_h(c + 1)
+            place(c)
         nc.sync.dma_start(out=out, in_=placed[:])

@@ -24,7 +24,7 @@ LIST_ROWS = 16
 SCALE_ROWS = 4
 CHUNK = 128
 CHUNKS = S // CHUNK
-WEAVE_ON_VECTOR = (384, 352)
+WEAVE_ON_VECTOR = (384, 320)
 BACK_ON_VECTOR = 32
 
 
@@ -64,6 +64,13 @@ def tile_picked_route2_glusilu_e_kernel(
                 nc.sync.dma_start(out=x_rows[g, u][:], in_=pass_rows(xT, g)[:, 2 * u : 2 * u + 2, :])
                 if (g, u) == (0, 0):
                     nc.sync.dma_start(picks[:], offs)
+                if (g, u) == (0, 1):
+                    for quadrant in range(P // 32):
+                        rows = slice(SCALE_ROWS * quadrant, SCALE_ROWS * (quadrant + 1))
+                        nc.sync.dma_start(
+                            out=w2_plane[32 * quadrant : 32 * quadrant + SCALE_ROWS, :].bitcast(I32),
+                            in_=w2_scales[0, rows, :].bitcast(I32),
+                        )
         whole = (0, PACK * H)
         w1_raw = [load_weight("w1_raw%d" % g, w1, g, whole) for g in range(PASSES)]
         w3_raw_first = load_weight("w3_raw0", w3, 0, whole)
@@ -76,11 +83,6 @@ def tile_picked_route2_glusilu_e_kernel(
         nc.sync.dma_start(out=gates[:], in_=gate)
         places = keep.tile([P, S // LIST_ROWS], U16, name="places")
         nc.sync.dma_start(places[:], dst)
-        for quadrant in range(P // 32):
-            nc.gpsimd.dma_start(
-                out=w2_plane[32 * quadrant : 32 * quadrant + SCALE_ROWS, :].bitcast(I32),
-                in_=w2_scales[0, SCALE_ROWS * quadrant : SCALE_ROWS * (quadrant + 1), :].bitcast(I32),
-            )
 
         def weight_tiles(name):
             words = keep.tile([P, H], U32, name=name + "_codes", align_bytes=64)
@@ -176,9 +178,8 @@ def tile_picked_route2_glusilu_e_kernel(
             return acc
 
         dealt = dealt_pairs("w1_bf1", P, back="other_back")
-        deal(nc.scalar.copy, dealt, w1_raw[1], 1, slice(BACK_ON_VECTOR, P))
+        deal(nc.scalar.copy, dealt, w1_raw[1], 1, slice(0, P))
         deal(nc.vector.tensor_copy, dealt, w1_raw[1], 0, slice(0, P))
-        deal(nc.vector.tensor_copy, dealt, w1_raw[1], 1, slice(0, BACK_ON_VECTOR))
         for tiles in ((0, 1), (2, 3)):
             quantize_weight(w1_q[1], dealt, tiles)
         a_acc = [first_layer("a_acc", c, w1_q, c, (0, 1) if c < CHUNKS // 2 else (1, 0)) for c in range(CHUNKS)]
@@ -204,7 +205,7 @@ def tile_picked_route2_glusilu_e_kernel(
         deal(nc.scalar.copy, dealt, w3_raw_last, 1, slice(middle + BACK_ON_VECTOR, P))
         deal(nc.vector.tensor_copy, dealt, w3_raw_last, 0, slice(middle, P))
         deal(nc.vector.tensor_copy, dealt, w3_raw_last, 1, slice(middle, middle + BACK_ON_VECTOR))
-        for tiles in ((0, 1), (2, 3)):
+        for tiles in ((0, 1), (2,), (3,)):
             quantize_weight(w3_q[1], dealt, tiles)
         silu_rest = keep.tile([P, CHUNKS - 1, CHUNK, PACK], F32, name="silu_rest", tag="w3_raw1")
         for c in range(1, CHUNKS):

@@ -226,9 +226,9 @@ def tile_picked_route2_glusilu_e_kernel(
             width = CHUNK if c == 0 else CHUNK // 2
             for lo in range(0, CHUNK, width):
                 nc.vector.tensor_tensor(
-                    h_bf[:, c * CHUNK + lo : c * CHUNK + lo + width, :],
-                    b_acc[:, :, lo : lo + width].rearrange("p t n -> p n t"),
-                    silu_a[c][:, lo : lo + width, :],
+                    h_bf[:, c * CHUNK + lo : c * CHUNK + lo + width, :].rearrange("p (n i) t -> p n t i", i=2),
+                    b_acc[:, :, lo : lo + width].rearrange("p t (n i) -> p n t i", i=2),
+                    silu_a[c][:, lo : lo + width, :].rearrange("p (n i) t -> p n t i", i=2),
                     MULT,
                 )
 

@@ -254,7 +254,11 @@ def tile_picked_route2_glusilu_e_kernel(
             cols = entries_of(c)
             nc.vector.tensor_tensor(gated[c][:], y_acc[c][:], gates[:, cols], MULT)
             entries = slice(cols.start // LIST_ROWS, cols.stop // LIST_ROWS)
-            nc.scalar.activation(placed[:].indirect(places[:, entries]), gated[c][:], COPY)
+            target = placed[:].indirect(places[:, entries])
+            if c + 1 < CHUNKS:
+                nc.scalar.activation(target, gated[c][:], COPY)
+            else:
+                nc.vector.tensor_copy(target, gated[c][:])
 
         make_h(0)
         for c in range(CHUNKS):

@@ -187,7 +187,7 @@ def tile_picked_route2_glusilu_e_kernel(
         silu_a = []
 
         def silu(c):
-            nc.scalar.activation(silu_a[c], a_acc[c][:].rearrange("p t n -> p n t"), SILU)
+            nc.scalar.activation(silu_a[c], a_acc[c][:].rearrange("p t (n i) -> p n t i", i=2), SILU)
 
         dealt = dealt_pairs("w3_bf0", P)
         deal(nc.scalar.copy, dealt, w3_raw_first, 1, slice(BACK_ON_VECTOR, P))
@@ -195,7 +195,7 @@ def tile_picked_route2_glusilu_e_kernel(
         deal(nc.vector.tensor_copy, dealt, w3_raw_first, 1, slice(0, BACK_ON_VECTOR))
         for tiles in ((0, 1), (2, 3)):
             quantize_weight(w3_q[0], dealt, tiles)
-        silu_first = keep.tile([P, CHUNK, PACK], F32, name="silu_first", tag="w3_raw0")
+        silu_first = keep.tile([P, CHUNK // 2, PACK, 2], F32, name="silu_first", tag="w3_raw0")
         silu_a.append(silu_first[:])
         silu(0)
         dealt = dealt_pairs("w3_bf1", P, back="other_back")
@@ -207,9 +207,9 @@ def tile_picked_route2_glusilu_e_kernel(
         deal(nc.vector.tensor_copy, dealt, w3_raw_last, 1, slice(middle, middle + BACK_ON_VECTOR))
         for tiles in ((0, 1), (2,), (3,)):
             quantize_weight(w3_q[1], dealt, tiles)
-        silu_rest = keep.tile([P, CHUNKS - 1, CHUNK, PACK], F32, name="silu_rest", tag="w3_raw1")
+        silu_rest = keep.tile([P, CHUNKS - 1, CHUNK // 2, PACK, 2], F32, name="silu_rest", tag="w3_raw1")
         for c in range(1, CHUNKS):
-            silu_a.append(silu_rest[:, c - 1, :, :])
+            silu_a.append(silu_rest[:, c - 1, :, :, :])
             silu(c)
 
         h_bf = keep.tile([P, S, PACK], BF16, name="h_bf", align_bytes=64)
@@ -228,7 +228,7 @@ def tile_picked_route2_glusilu_e_kernel(
                 nc.vector.tensor_tensor(
                     h_bf[:, c * CHUNK + lo : c * CHUNK + lo + width, :].rearrange("p (n i) t -> p n t i", i=2),
                     b_acc[:, :, lo : lo + width].rearrange("p t (n i) -> p n t i", i=2),
-                    silu_a[c][:, lo : lo + width, :].rearrange("p (n i) t -> p n t i", i=2),
+                    silu_a[c][:, lo // 2 : (lo + width) // 2, :, :],
                     MULT,
                 )
 

@@ -96,10 +96,10 @@ def tile_picked_route2_glusilu_e_kernel(
             ]
 
         def deal(copy, dealt, raw, pair, ms, m0=0):
-            columns = raw[:, :, PACK * ms.start : PACK * ms.stop].rearrange("p j (m i t) -> p m j t i", i=2, t=PACK)
+            columns = raw[:, :, PACK * ms.start : PACK * ms.stop].rearrange("p j (m i t) -> p m j i t", i=2, t=PACK)
             copy(
-                dealt[pair][:, :, ms.start - m0 : ms.stop - m0, :].rearrange("p t (m i) j -> p m j t i", i=2),
-                columns[:, :, :, 2 * pair : 2 * pair + 2, :],
+                dealt[pair][:, :, ms.start - m0 : ms.stop - m0, :].rearrange("p t (m i) j -> p m j i t", i=2),
+                columns[:, :, :, :, 2 * pair : 2 * pair + 2],
             )
 
         def quantize_weight(w_pass, dealt, tiles, m0=0):

from contextlib import ExitStack

import concourse.mybir as mybir

K, T, S, H, N, U = 1024, 1024, 512, 512, 128, 1024
FLOPS = 2 * S * (2 * K * H + H * N)

F32 = mybir.dt.float32
BF16 = mybir.dt.bfloat16
I32 = mybir.dt.int32
U32 = mybir.dt.uint32
U16 = mybir.dt.uint16
U8 = mybir.dt.uint8
FP8X4 = mybir.dt.float8_e4m3fn_x4
MULT = mybir.AluOpType.mult
SILU = mybir.ActivationFunctionType.Silu
COPY = mybir.ActivationFunctionType.Copy

P = 128
PACK = 4
K_PASS = P * PACK
PASSES = K // K_PASS
LIST_ROWS = 16
SCALE_ROWS = 4
CHUNK = 128
CHUNKS = S // CHUNK
WEAVE_ON_VECTOR = (384, 320)
BACK_ON_VECTOR = 32


def tile_picked_route2_glusilu_e_kernel(
    tc, xT, gate, w1, w3, w2_words, w2_scales, offs, dst, out
):
    nc = tc.nc
    with ExitStack() as ctx:
        keep = ctx.enter_context(tc.tile_pool(name="keep", bufs=1))
        psum = ctx.enter_context(tc.psum_pool(name="psum", bufs=1))

        def pass_rows(matrix, g):
            return matrix[g * K_PASS : (g + 1) * K_PASS, :].rearrange("(p j) c -> p j c", j=PACK)

        def load_weight(name, matrix, g, cuts):
            raw = keep.tile([P, PACK * H], F32, name=name, tag=name)
            run = pass_rows(matrix, g).rearrange("p j c -> p (j c)")
            for lo, hi in zip(cuts[:-1], cuts[1:]):
                nc.sync.dma_start(out=raw[:, lo:hi], in_=run[:, lo:hi])
            return raw[:].rearrange("p (j c) -> p j c", j=PACK)

        warm = keep.tile([P, 8], F32, name="warm")
        nc.vector.memset(warm[:], 0.0)
        nc.scalar.activation(warm[:, 4:8], warm[:, 0:4], SILU)

        w2_plane = keep.tile([P, N], U8, name="w2_plane", align_bytes=64)
        nc.vector.memset(w2_plane[:], 0)
        placed = keep.tile([P, U], F32, name="placed")
        nc.vector.memset(placed[:], 0.0)

        x_rows = {}
        picks = keep.tile([P, S // LIST_ROWS], U16, name="picks")
        for g in range(PASSES):
            for u in range(2):
                label = "x_rows%d%d" % (g, u)
                x_rows[g, u] = keep.tile([P, 2, T], F32, name=label, tag=label, align_bytes=64)
                nc.sync.dma_start(out=x_rows[g, u][:], in_=pass_rows(xT, g)[:, 2 * u : 2 * u + 2, :])
                if (g, u) == (0, 0):
                    nc.sync.dma_start(picks[:], offs)
                if (g, u) == (0, 1):
                    for quadrant in range(P // 32):
                        rows = slice(SCALE_ROWS * quadrant, SCALE_ROWS * (quadrant + 1))
                        nc.sync.dma_start(
                            out=w2_plane[32 * quadrant : 32 * quadrant + SCALE_ROWS, :].bitcast(I32),
                            in_=w2_scales[0, rows, :].bitcast(I32),
                        )
        whole = (0, PACK * H)
        w1_raw = [load_weight("w1_raw%d" % g, w1, g, whole) for g in range(PASSES)]
        w3_raw_first = load_weight("w3_raw0", w3, 0, whole)
        w3_raw_last = load_weight("w3_raw1", w3, 1, (0, PACK * H - H // 2, PACK * H))
        w2_codes = keep.tile([P, N], U32, name="w2_codes", align_bytes=64)
        nc.sync.dma_start(
            out=w2_codes[:].bitcast(I32), in_=w2_words[0].rearrange("p n t -> p (n t)").bitcast(I32)
        )
        gates = keep.tile([P, S], F32, name="gates")
        nc.sync.dma_start(out=gates[:], in_=gate)
        places = keep.tile([P, S // LIST_ROWS], U16, name="places")
        nc.sync.dma_start(places[:], dst)

        def weight_tiles(name):
            words = keep.tile([P, H], U32, name=name + "_codes", align_bytes=64)
            scales = keep.tile([P, H], U8, name=name + "_scales", align_bytes=64)
            return words, scales

        def dealt_pairs(name, width, front="front", back="back"):
            return [
                keep.tile([P, 2, width, PACK], BF16, name=name + side, tag=place, align_bytes=64)
                for side, place in (("_front", front), ("_back", back))
            ]

        def deal(copy, dealt, raw, pair, ms, m0=0):
            columns = raw[:, :, PACK * ms.start : PACK * ms.stop].rearrange("p j (m i t) -> p m j i t", i=2, t=PACK)
            copy(
                dealt[pair][:, :, ms.start - m0 : ms.stop - m0, :].rearrange("p t (m i) j -> p m j i t", i=2),
                columns[:, :, :, :, 2 * pair : 2 * pair + 2],
            )

        def quantize_weight(w_pass, dealt, tiles, m0=0):
            words, scales = w_pass
            rounded = dealt[tiles[0] // 2][:, tiles[0] % 2 : tiles[-1] % 2 + 1, :, :]
            lo = tiles[0] * P + m0
            hi = lo + len(tiles) * rounded.shape[2]
            nc.vector.quantize_mx(
                out=words[:, lo:hi].bitcast(FP8X4),
                scales=scales[:, lo:hi],
                in_=rounded.rearrange("p t m j -> p (t m j)"),
            )

        planes = [keep.tile([P, PACK, S], F32, name="planes%d" % g) for g in range(PASSES)]
        picked = [keep.tile([P, S, PACK], BF16, name="picked%d" % g, align_bytes=64) for g in range(PASSES)]
        picked_codes = []
        picked_scales = []

        def gather(g, u):
            nc.scalar.activation(planes[g][:, 2 * u, :], x_rows[g, u][:, 0, :].indirect(picks[:]), COPY)
            nc.vector.tensor_copy(planes[g][:, 2 * u + 1, :], x_rows[g, u][:, 1, :].indirect(picks[:]))

        def weave(g):
            on_vector = WEAVE_ON_VECTOR[g]
            for copy, part in (
                (nc.scalar.copy, slice(on_vector, S)),
                (nc.vector.tensor_copy, slice(0, on_vector)),
            ):
                copy(
                    picked[g][:, part, :].rearrange("p (c i) j -> p c j i", i=4),
                    planes[g][:, :, part].rearrange("p j (c i) -> p c j i", i=4),
                )

        def quantize_tokens(g, place):
            codes = keep.tile([P, S], U32, name="picked_codes%d" % g, tag=place, align_bytes=64)
            scales = keep.tile([P, S], U8, name="picked_scales%d" % g, align_bytes=64)
            nc.vector.quantize_mx(
                out=codes[:].bitcast(FP8X4), scales=scales[:], in_=picked[g][:].rearrange("p s j -> p (s j)")
            )
            picked_codes.append(codes)
            picked_scales.append(scales)

        gather(0, 0)
        gather(0, 1)
        weave(0)
        gather(1, 0)
        quantize_tokens(0, "x_rows10")
        gather(1, 1)
        weave(1)
        w1_dealt = dealt_pairs("w1_bf0", P)
        deal(nc.scalar.copy, w1_dealt, w1_raw[0], 1, slice(0, P))
        deal(nc.vector.tensor_copy, w1_dealt, w1_raw[0], 0, slice(0, P))
        quantize_tokens(1, "picked_codes1")

        w1_q = [weight_tiles("w1_%d" % g) for g in range(PASSES)]
        w3_q = [weight_tiles("w3_%d" % g) for g in range(PASSES)]
        for tiles in ((0, 1), (2, 3)):
            quantize_weight(w1_q[0], w1_dealt, tiles)

        def first_layer(name, bank, w_q, c, passes=(0, 1)):
            cols = slice(c * CHUNK, (c + 1) * CHUNK)
            acc = psum.tile([P, PACK, CHUNK], F32, name="%s%d" % (name, c), tag="bank%d" % bank)
            for g in passes:
                tiles = range(PACK) if g == 0 or c == 0 else range(PACK - 1, -1, -1)
                for t in tiles:
                    words, scales = w_q[g]
                    nc.tensor.matmul_mx(
                        out=acc[:, t, :],
                        lhsT=words[:, t * P : (t + 1) * P].bitcast(FP8X4),
                        lhsT_scale=scales[:, t * P : (t + 1) * P],
                        rhs=picked_codes[g][:, cols].bitcast(FP8X4),
                        rhs_scale=picked_scales[g][:, cols],
                        start=(g == passes[0] and t == tiles[0]),
                        stop=(g == passes[-1] and t == tiles[-1]),
                    )
            return acc

        dealt = dealt_pairs("w1_bf1", P, back="other_back")
        deal(nc.scalar.copy, dealt, w1_raw[1], 1, slice(0, P))
        deal(nc.vector.tensor_copy, dealt, w1_raw[1], 0, slice(0, P))
        for tiles in ((0, 1), (2, 3)):
            quantize_weight(w1_q[1], dealt, tiles)
        a_acc = [first_layer("a_acc", c, w1_q, c, (0, 1) if c < CHUNKS // 2 else (1, 0)) for c in range(CHUNKS)]

        silu_a = []

        def silu(c):
            nc.scalar.activation(silu_a[c], a_acc[c][:].rearrange("p t (n i) -> p n t i", i=2), SILU)

        dealt = dealt_pairs("w3_bf0", P)
        deal(nc.scalar.copy, dealt, w3_raw_first, 1, slice(BACK_ON_VECTOR, P))
        deal(nc.vector.tensor_copy, dealt, w3_raw_first, 0, slice(0, P))
        deal(nc.vector.tensor_copy, dealt, w3_raw_first, 1, slice(0, BACK_ON_VECTOR))
        for tiles in ((0, 1), (2, 3)):
            quantize_weight(w3_q[0], dealt, tiles)
        silu_first = keep.tile([P, CHUNK // 2, PACK, 2], F32, name="silu_first", tag="w3_raw0")
        silu_a.append(silu_first[:])
        silu(0)
        dealt = dealt_pairs("w3_bf1", P, back="other_back")
        middle = P // 2
        deal(nc.scalar.copy, dealt, w3_raw_last, 1, slice(0, middle))
        deal(nc.vector.tensor_copy, dealt, w3_raw_last, 0, slice(0, middle))
        deal(nc.scalar.copy, dealt, w3_raw_last, 1, slice(middle + BACK_ON_VECTOR, P))
        deal(nc.vector.tensor_copy, dealt, w3_raw_last, 0, slice(middle, P))
        deal(nc.vector.tensor_copy, dealt, w3_raw_last, 1, slice(middle, middle + BACK_ON_VECTOR))
        for tiles in ((0, 1), (2,), (3,)):
            quantize_weight(w3_q[1], dealt, tiles)
        silu_rest = keep.tile([P, CHUNKS - 1, CHUNK // 2, PACK, 2], F32, name="silu_rest", tag="w3_raw1")
        for c in range(1, CHUNKS):
            silu_a.append(silu_rest[:, c - 1, :, :, :])
            silu(c)

        h_bf = keep.tile([P, S, PACK], BF16, name="h_bf", align_bytes=64)
        h_codes = keep.tile([P, S], U32, name="h_codes", align_bytes=64)
        h_scales = keep.tile([P, S], U8, name="h_scales", align_bytes=64)
        gated = [keep.tile([P, CHUNK], F32, name="gated%d" % c) for c in range(CHUNKS)]
        y_acc = {}

        def entries_of(c):
            return slice(c * CHUNK, (c + 1) * CHUNK)

        def make_h(c):
            b_acc = first_layer("b_acc", CHUNKS + c, w3_q, c, (0, 1) if c < CHUNKS // 2 else (1, 0))
            width = CHUNK if c == 0 else CHUNK // 2
            for lo in range(0, CHUNK, width):
                nc.vector.tensor_tensor(
                    h_bf[:, c * CHUNK + lo : c * CHUNK + lo + width, :].rearrange("p (n i) t -> p n t i", i=2),
                    b_acc[:, :, lo : lo + width].rearrange("p t (n i) -> p n t i", i=2),
                    silu_a[c][:, lo // 2 : (lo + width) // 2, :, :],
                    MULT,
                )

        def second_layer(c):
            cols = entries_of(c)
            nc.vector.quantize_mx(
                out=h_codes[:, cols].bitcast(FP8X4),
                scales=h_scales[:, cols],
                in_=h_bf[:, cols, :].rearrange("p n t -> p (n t)"),
            )
            y_acc[c] = psum.tile([P, CHUNK], F32, name="y_acc%d" % c, tag="bank%d" % c)
            nc.tensor.matmul_mx(
                out=y_acc[c][:],
                lhsT=w2_codes[:].bitcast(FP8X4),
                lhsT_scale=w2_plane[:],
                rhs=h_codes[:, cols].bitcast(FP8X4),
                rhs_scale=h_scales[:, cols],
                start=True,
                stop=True,
            )

        def place(c):
            cols = entries_of(c)
            nc.vector.tensor_tensor(gated[c][:], y_acc[c][:], gates[:, cols], MULT)
            entries = slice(cols.start // LIST_ROWS, cols.stop // LIST_ROWS)
            target = placed[:].indirect(places[:, entries])
            if c + 1 < CHUNKS:
                nc.scalar.activation(target, gated[c][:], COPY)
            else:
                nc.vector.tensor_copy(target, gated[c][:])

        make_h(0)
        for c in range(CHUNKS):
            second_layer(c)
            if c + 1 < CHUNKS:
                make_h(c + 1)
            place(c)
        nc.sync.dma_start(out=out, in_=placed[:])
